import numpy as np
import ml_dtypes


def mxq(x, axis, fmt="e4m3"):
    dtype, down = {"e4m3": (ml_dtypes.float8_e4m3fn, 7), "e5m2": (ml_dtypes.float8_e5m2, 14)}[fmt]
    v = np.moveaxis(np.asarray(x, np.float32).astype(ml_dtypes.bfloat16).astype(np.float64), axis, -1)
    blocks = v.reshape(v.shape[:-1] + (-1, 32))
    amax = np.abs(blocks).max(-1, keepdims=True)
    byte = np.maximum(np.where(amax > 0, np.frexp(amax)[1] - 1 + 127, 0) - down, 1)
    scale = np.exp2(byte - 127.0)
    codes = (blocks / scale).astype(np.float32).astype(dtype).astype(np.float64)
    return np.moveaxis((codes * scale).reshape(v.shape), -1, axis)


WIDE = False


def mx_kscale(k):
    if not WIDE:
        return np.ones(k)
    levels = np.array([10, -10, 5, -5, 0])
    if k % 512:
        return np.exp2(np.random.permutation(np.resize(levels, k // 32))).repeat(32)
    a = np.empty((k // 512, 16))
    for p in range(k // 512):
        a[p, :8] = np.random.permutation(np.resize(levels, 8))
        for g in range(8):
            far = levels[np.abs(levels - a[p, g]) >= 10]
            a[p, g + 8] = far[np.random.randint(len(far))]
    return np.exp2(a.ravel()).repeat(32)


def f64(x):
    return np.asarray(x).astype(np.float64)


def striped(idx):
    return np.tile(np.asarray(idx).reshape(-1, 16).T, (8, 1)).astype(np.uint16)


def unstriped(offs):
    return offs[:16].T.reshape(-1).astype(np.int64)


E2M1 = np.array([0.0, 0.5, 1.0, 1.5, 2.0, 3.0, 4.0, 6.0, -0.0, -0.5, -1.0, -1.5, -2.0, -3.0, -4.0, -6.0])


def pack_weight(w, fmt):
    k, n = w.shape
    w = f64(np.asarray(w, np.float32).astype(ml_dtypes.bfloat16)).reshape(k // 32, 32, n)
    amax = np.abs(w).max(1)
    if fmt == "e4m3":
        byte = np.frexp(amax)[1] - 1 + 127 - 7
    else:
        mant, ex = np.frexp(amax / 6.0)
        byte = np.where(mant > 0.5, ex, ex - 1) + 127
    byte = np.clip(np.where(amax > 0, byte, 1), 1, 254)
    scaled = (w * np.exp2(127.0 - byte)[:, None, :]).reshape(k, n).astype(np.float32)
    by_word = np.ascontiguousarray(scaled.reshape(k // 512, 128, 4, n).transpose(0, 1, 3, 2))
    if fmt == "e4m3":
        words = by_word.astype(ml_dtypes.float8_e4m3fn).view(np.uint8)
    else:
        c = by_word.astype(ml_dtypes.float4_e2m1fn).view(np.uint8) & 0xF
        words = (c[..., 0::2] | (c[..., 1::2] << 4)).reshape(k // 512, 128, 2 * n)
    return np.ascontiguousarray(words), np.ascontiguousarray(byte.astype(np.uint8).reshape(k // 512, 16, n))


def unpack_weight(words, scales, fmt):
    g, _, n = scales.shape
    words = np.ascontiguousarray(words).reshape(g, 128, n, -1)
    if fmt == "e4m3":
        vals = words.view(ml_dtypes.float8_e4m3fn).astype(np.float64)
    else:
        nib = np.empty((g, 128, n, 4), np.uint8)
        nib[..., 0::2] = words & 0xF
        nib[..., 1::2] = words >> 4
        vals = E2M1[nib]
    vals = vals * np.repeat(np.exp2(scales.astype(np.float64) - 127.0), 8, axis=1)[..., None]
    return vals.transpose(0, 1, 3, 2).reshape(g * 512, n)


B, N, T, D, NQ = 1, 512, 2048, 512, 256


def setup_inputs():
    n = np.random.standard_normal
    idx = np.random.permutation(T)[:B * N]
    s = mx_kscale(D)[:, None]
    mid = n((D, T))
    kp = pack_weight((mid + np.abs(n((D, T)))) / s, "e4m3")
    cp = pack_weight((mid - np.abs(n((D, T)))) / s, "e4m3")
    return {
        "qT": (n((B, D, NQ)) * s * (1.00 / np.sqrt(D))).astype(np.float32),
        "k_words": kp[0],
        "k_scales": kp[1],
        "c_words": cp[0],
        "c_scales": cp[1],
        "offs": striped(idx),
    }


def reference(qT, k_words, k_scales, c_words, c_scales, offs):
    idx = unstriped(offs)
    pick = lambda x, which: x[:, which].reshape(x.shape[0], B, -1).transpose(1, 0, 2)
    k = unpack_weight(k_words, k_scales, "e4m3")
    kg = pick(k, idx)
    c = unpack_weight(c_words, c_scales, "e4m3")
    cg = pick(c, idx)
    hiq = mxq(np.maximum(f64(qT), 0.0), 1, "e4m3")
    loq = mxq(np.minimum(f64(qT), 0.0), 1, "e4m3")
    a = (hiq.transpose(0, 2, 1) @ kg) + (loq.transpose(0, 2, 1) @ cg)
    return a

@@ -1,0 +1,107 @@
+from contextlib import ExitStack
+
+import concourse.mybir as mybir
+
+D, NQ, T, N = 512, 256, 2048, 512
+FLOPS = 2 * 2 * D * NQ * N
+
+F32 = mybir.dt.float32
+BF16 = mybir.dt.bfloat16
+I32 = mybir.dt.int32
+U32 = mybir.dt.uint32
+U16 = mybir.dt.uint16
+U8 = mybir.dt.uint8
+FP8X4 = mybir.dt.float8_e4m3fn_x4
+
+P = 128
+PACK = 4
+ROWS = 16
+HALF = N // 2
+LIST_COLS = N // 16
+
+
+def tile_attend_quest_topk_kernel(tc, qT, k_words, k_scales, c_words, c_scales, offs, out):
+    nc = tc.nc
+    with ExitStack() as ctx:
+        keep = ctx.enter_context(tc.tile_pool(name="keep", bufs=1))
+        psum = ctx.enter_context(tc.psum_pool(name="psum", bufs=1))
+
+        offsets = keep.tile([P, LIST_COLS], U16, name="offsets")
+        ks_pool = keep.tile([P, T], U8, name="ks_pool", align_bytes=64)
+        cs_pool = keep.tile([P, T], U8, name="cs_pool", align_bytes=64)
+        q_raw = keep.tile([P, PACK * NQ], F32, name="q_raw", align_bytes=64)
+        kw_pool = keep.tile([P, T], I32, name="kw_pool", tag="kw", align_bytes=64)
+        cw_pool = keep.tile([P, T], I32, name="cw_pool", align_bytes=64)
+
+        nc.vector.memset(ks_pool[:].bitcast(I32), 0)
+        nc.vector.memset(cs_pool[:].bitcast(I32), 0)
+        nc.sync.dma_start(offsets[:], offs)
+        nc.scalar.dma_start(ks_pool[0:ROWS, :].bitcast(I32), k_scales[0].bitcast(I32))
+        nc.scalar.dma_start(cs_pool[0:ROWS, :].bitcast(I32), c_scales[0].bitcast(I32))
+        nc.sync.dma_start(q_raw[:], qT[0].rearrange("(p j) w -> p (j w)", j=PACK))
+        nc.sync.dma_start(kw_pool[:], k_words[0].rearrange("p t r -> p (t r)").bitcast(I32))
+        nc.sync.dma_start(cw_pool[:], c_words[0].rearrange("p t r -> p (t r)").bitcast(I32))
+
+        ks_got = keep.tile([P, N], U8, name="ks_got", tag="ks", align_bytes=64)
+        cs_got = keep.tile([P, N], U8, name="cs_got", tag="cs", align_bytes=64)
+        planes = keep.tile([P, 2 * N], U8, name="planes", align_bytes=64)
+        nc.vector.tensor_copy(ks_got[:], ks_pool[:].indirect(offsets[:]))
+        nc.vector.tensor_copy(cs_got[:], cs_pool[:].indirect(offsets[:]))
+        nc.vector.tensor_copy(planes[:, 0:N].bitcast(I32), ks_got[:].bitcast(I32))
+        nc.vector.tensor_copy(planes[:, N : 2 * N].bitcast(I32), cs_got[:].bitcast(I32))
+        for quad in range(1, 4):
+            nc.scalar.dma_start(
+                planes[32 * quad : 32 * quad + 4, :].bitcast(I32), planes[4 * quad : 4 * quad + 4, :].bitcast(I32)
+            )
+
+        hi = keep.tile([P, NQ * PACK], BF16, name="hi", tag="hi", align_bytes=64)
+        lo = keep.tile([P, NQ * PACK], BF16, name="lo", tag="ks", align_bytes=64)
+        q_walk = q_raw[:].rearrange("p (t c i) -> p c t i", t=PACK, i=4)
+        nc.scalar.activation(
+            hi[:].rearrange("p (c i t) -> p c t i", t=PACK, i=4), q_walk, mybir.ActivationFunctionType.Relu
+        )
+        nc.vector.tensor_scalar_min(lo[:].rearrange("p (c i t) -> p c t i", t=PACK, i=4), q_walk, 0.0)
+        hi_codes = keep.tile([P, NQ], U32, name="hi_codes", tag="cs", align_bytes=64)
+        lo_codes = keep.tile([P, NQ], U32, name="lo_codes", align_bytes=64)
+        hi_scales = keep.tile([P, NQ], U8, name="hi_scales", align_bytes=64)
+        lo_scales = keep.tile([P, NQ], U8, name="lo_scales", align_bytes=64)
+        nc.vector.quantize_mx(out=hi_codes[:].bitcast(FP8X4), scales=hi_scales[:], in_=hi[:])
+        nc.vector.quantize_mx(out=lo_codes[:].bitcast(FP8X4), scales=lo_scales[:], in_=lo[:])
+
+        banks = {}
+        for half in range(2):
+            for tile in range(2):
+                banks[half, tile] = psum.tile([P, HALF], F32, name="bank%d%d" % (half, tile))
+
+        for table, pool, codes, scales, tag in (
+            (0, kw_pool, hi_codes, hi_scales, "hi"),
+            (1, cw_pool, lo_codes, lo_scales, "kw"),
+        ):
+            both = keep.tile([P, N], U32, name="got%d" % table, tag=tag, align_bytes=64)
+            for half in range(2):
+                got = both[:, half * HALF : (half + 1) * HALF]
+                part = offsets[:, half * LIST_COLS // 2 : (half + 1) * LIST_COLS // 2]
+                nc.vector.tensor_copy(got, pool[:].bitcast(U32).indirect(part))
+                first = table * N + half * HALF
+                for tile in range(2):
+                    rows = slice(tile * P, (tile + 1) * P)
+                    nc.tensor.matmul_mx(
+                        out=banks[half, tile][:],
+                        lhsT=codes[:, rows].bitcast(FP8X4),
+                        lhsT_scale=scales[:, rows],
+                        rhs=got.bitcast(FP8X4),
+                        rhs_scale=planes[:, first : first + HALF],
+                        start=(table == 0),
+                        stop=(table == 1),
+                    )
+
+        early = keep.tile([P, 2, HALF], F32, name="early")
+        for tile in range(2):
+            nc.scalar.copy(early[:, tile, :], banks[0, tile][:])
+        nc.sync.dma_start(out[0].rearrange("(t p) n -> p t n", p=P)[:, :, 0:HALF], early[:])
+        late0 = keep.tile([P, HALF], F32, name="late0")
+        nc.vector.tensor_copy(late0[:], banks[1, 0][:])
+        nc.sync.dma_start(out[0, 0:P, HALF:N], late0[:])
+        late1 = keep.tile([P, HALF], F32, name="late1")
+        nc.scalar.copy(late1[:], banks[1, 1][:])
+        nc.scalar.dma_start(out[0, P:NQ, HALF:N], late1[:])

@@ -22,6 +22,7 @@ LIST_COLS = N // 16
 
 def tile_attend_quest_topk_kernel(tc, qT, k_words, k_scales, c_words, c_scales, offs, out):
     nc = tc.nc
+    relu = mybir.ActivationFunctionType.Relu
     with ExitStack() as ctx:
         keep = ctx.enter_context(tc.tile_pool(name="keep", bufs=1))
         psum = ctx.enter_context(tc.psum_pool(name="psum", bufs=1))
@@ -30,42 +31,48 @@ def tile_attend_quest_topk_kernel(tc, qT, k_words, k_scales, c_words, c_scales, 
         ks_pool = keep.tile([P, T], U8, name="ks_pool", align_bytes=64)
         cs_pool = keep.tile([P, T], U8, name="cs_pool", align_bytes=64)
         q_raw = keep.tile([P, PACK * NQ], F32, name="q_raw", align_bytes=64)
-        kw_pool = keep.tile([P, T], I32, name="kw_pool", tag="kw", align_bytes=64)
+        kw_pool = keep.tile([P, T], I32, name="kw_pool", align_bytes=64)
         cw_pool = keep.tile([P, T], I32, name="cw_pool", align_bytes=64)
 
-        nc.vector.memset(ks_pool[:].bitcast(I32), 0)
-        nc.vector.memset(cs_pool[:].bitcast(I32), 0)
+        top = P - ROWS
+        nc.sync.dma_start(ks_pool[top:P, :].bitcast(I32), k_scales[0].bitcast(I32))
         nc.sync.dma_start(offsets[:], offs)
-        nc.scalar.dma_start(ks_pool[0:ROWS, :].bitcast(I32), k_scales[0].bitcast(I32))
-        nc.scalar.dma_start(cs_pool[0:ROWS, :].bitcast(I32), c_scales[0].bitcast(I32))
+        nc.sync.dma_start(cs_pool[top:P, :].bitcast(I32), c_scales[0].bitcast(I32))
         nc.sync.dma_start(q_raw[:], qT[0].rearrange("(p j) w -> p (j w)", j=PACK))
         nc.sync.dma_start(kw_pool[:], k_words[0].rearrange("p t r -> p (t r)").bitcast(I32))
         nc.sync.dma_start(cw_pool[:], c_words[0].rearrange("p t r -> p (t r)").bitcast(I32))
+        nc.vector.memset(ks_pool[0:top, :].bitcast(I32), 0)
+        nc.vector.memset(cs_pool[0:top, :].bitcast(I32), 0)
 
-        ks_got = keep.tile([P, N], U8, name="ks_got", tag="ks", align_bytes=64)
-        cs_got = keep.tile([P, N], U8, name="cs_got", tag="cs", align_bytes=64)
+        ks_got = keep.tile([P, N], U8, name="ks_got", align_bytes=64)
+        cs_got = keep.tile([P, N], U8, name="cs_got", align_bytes=64)
         planes = keep.tile([P, 2 * N], U8, name="planes", align_bytes=64)
         nc.vector.tensor_copy(ks_got[:], ks_pool[:].indirect(offsets[:]))
         nc.vector.tensor_copy(cs_got[:], cs_pool[:].indirect(offsets[:]))
         nc.vector.tensor_copy(planes[:, 0:N].bitcast(I32), ks_got[:].bitcast(I32))
         nc.vector.tensor_copy(planes[:, N : 2 * N].bitcast(I32), cs_got[:].bitcast(I32))
-        for quad in range(1, 4):
-            nc.scalar.dma_start(
-                planes[32 * quad : 32 * quad + 4, :].bitcast(I32), planes[4 * quad : 4 * quad + 4, :].bitcast(I32)
+        for quad in range(4):
+            nc.sync.dma_start(
+                planes[32 * quad : 32 * quad + 4, :].bitcast(I32),
+                planes[top + 4 * quad : top + 4 * quad + 4, :].bitcast(I32),
             )
 
-        hi = keep.tile([P, NQ * PACK], BF16, name="hi", tag="hi", align_bytes=64)
-        lo = keep.tile([P, NQ * PACK], BF16, name="lo", tag="ks", align_bytes=64)
+        hi = keep.tile([P, NQ * PACK], BF16, name="hi", align_bytes=64)
+        lo = keep.tile([P, NQ * PACK], BF16, name="lo", align_bytes=64)
         q_walk = q_raw[:].rearrange("p (t c i) -> p c t i", t=PACK, i=4)
-        nc.scalar.activation(
-            hi[:].rearrange("p (c i t) -> p c t i", t=PACK, i=4), q_walk, mybir.ActivationFunctionType.Relu
-        )
-        nc.vector.tensor_scalar_min(lo[:].rearrange("p (c i t) -> p c t i", t=PACK, i=4), q_walk, 0.0)
-        hi_codes = keep.tile([P, NQ], U32, name="hi_codes", tag="cs", align_bytes=64)
+        nc.scalar.activation(hi[:].rearrange("p (c i t) -> p c t i", t=PACK, i=4), q_walk, relu)
+        neg = keep.tile([P, NQ * PACK], F32, name="neg", align_bytes=64)
+        nc.scalar.activation(neg[:].rearrange("p (c i t) -> p c t i", t=PACK, i=4), q_walk, relu, scale=-1.0)
+        nc.scalar.mul(lo[:], neg[:], -1.0)
+
+        kw_got = keep.tile([P, N], U32, name="kw_got", align_bytes=64)
+        cw_got = keep.tile([P, N], U32, name="cw_got", align_bytes=64)
+        hi_codes = keep.tile([P, NQ], U32, name="hi_codes", align_bytes=64)
         lo_codes = keep.tile([P, NQ], U32, name="lo_codes", align_bytes=64)
         hi_scales = keep.tile([P, NQ], U8, name="hi_scales", align_bytes=64)
         lo_scales = keep.tile([P, NQ], U8, name="lo_scales", align_bytes=64)
         nc.vector.quantize_mx(out=hi_codes[:].bitcast(FP8X4), scales=hi_scales[:], in_=hi[:])
+        nc.vector.tensor_copy(kw_got[:], kw_pool[:].bitcast(U32).indirect(offsets[:]))
         nc.vector.quantize_mx(out=lo_codes[:].bitcast(FP8X4), scales=lo_scales[:], in_=lo[:])
 
         banks = {}
@@ -73,27 +80,26 @@ def tile_attend_quest_topk_kernel(tc, qT, k_words, k_scales, c_words, c_scales, 
             for tile in range(2):
                 banks[half, tile] = psum.tile([P, HALF], F32, name="bank%d%d" % (half, tile))
 
-        for table, pool, codes, scales, tag in (
-            (0, kw_pool, hi_codes, hi_scales, "hi"),
-            (1, cw_pool, lo_codes, lo_scales, "kw"),
-        ):
-            both = keep.tile([P, N], U32, name="got%d" % table, tag=tag, align_bytes=64)
-            for half in range(2):
-                got = both[:, half * HALF : (half + 1) * HALF]
-                part = offsets[:, half * LIST_COLS // 2 : (half + 1) * LIST_COLS // 2]
-                nc.vector.tensor_copy(got, pool[:].bitcast(U32).indirect(part))
-                first = table * N + half * HALF
-                for tile in range(2):
-                    rows = slice(tile * P, (tile + 1) * P)
-                    nc.tensor.matmul_mx(
-                        out=banks[half, tile][:],
-                        lhsT=codes[:, rows].bitcast(FP8X4),
-                        lhsT_scale=scales[:, rows],
-                        rhs=got.bitcast(FP8X4),
-                        rhs_scale=planes[:, first : first + HALF],
-                        start=(table == 0),
-                        stop=(table == 1),
-                    )
+        def passes(table, half, codes, scales, words):
+            first = table * N + half * HALF
+            for tile in range(2):
+                rows = slice(tile * P, (tile + 1) * P)
+                nc.tensor.matmul_mx(
+                    out=banks[half, tile][:],
+                    lhsT=codes[:, rows].bitcast(FP8X4),
+                    lhsT_scale=scales[:, rows],
+                    rhs=words[:, half * HALF : (half + 1) * HALF].bitcast(FP8X4),
+                    rhs_scale=planes[:, first : first + HALF],
+                    start=(table == 0),
+                    stop=(table == 1),
+                )
+
+        for half in range(2):
+            passes(0, half, hi_codes, hi_scales, kw_got)
+        for half in range(2):
+            part = offsets[:, half * LIST_COLS // 2 : (half + 1) * LIST_COLS // 2]
+            nc.vector.tensor_copy(cw_got[:, half * HALF : (half + 1) * HALF], cw_pool[:].bitcast(U32).indirect(part))
+            passes(1, half, lo_codes, lo_scales, cw_got)
 
         early = keep.tile([P, 2, HALF], F32, name="early")
         for tile in range(2):

@@ -35,7 +35,7 @@ def tile_attend_quest_topk_kernel(tc, qT, k_words, k_scales, c_words, c_scales, 
         cw_pool = keep.tile([P, T], I32, name="cw_pool", align_bytes=64)
 
         top = P - ROWS
-        nc.sync.dma_start(ks_pool[top:P, :].bitcast(I32), k_scales[0].bitcast(I32))
+        nc.scalar.dma_start(ks_pool[top:P, :].bitcast(I32), k_scales[0].bitcast(I32))
         nc.sync.dma_start(offsets[:], offs)
         nc.sync.dma_start(cs_pool[top:P, :].bitcast(I32), c_scales[0].bitcast(I32))
         nc.sync.dma_start(q_raw[:], qT[0].rearrange("(p j) w -> p (j w)", j=PACK))
@@ -44,26 +44,27 @@ def tile_attend_quest_topk_kernel(tc, qT, k_words, k_scales, c_words, c_scales, 
         nc.vector.memset(ks_pool[0:top, :].bitcast(I32), 0)
         nc.vector.memset(cs_pool[0:top, :].bitcast(I32), 0)
 
-        ks_got = keep.tile([P, N], U8, name="ks_got", align_bytes=64)
-        cs_got = keep.tile([P, N], U8, name="cs_got", align_bytes=64)
+        bytes_got = keep.tile([P, 2 * N], U8, name="bytes_got", align_bytes=64)
         planes = keep.tile([P, 2 * N], U8, name="planes", align_bytes=64)
-        nc.vector.tensor_copy(ks_got[:], ks_pool[:].indirect(offsets[:]))
-        nc.vector.tensor_copy(cs_got[:], cs_pool[:].indirect(offsets[:]))
-        nc.vector.tensor_copy(planes[:, 0:N].bitcast(I32), ks_got[:].bitcast(I32))
-        nc.vector.tensor_copy(planes[:, N : 2 * N].bitcast(I32), cs_got[:].bitcast(I32))
+        nc.vector.memset(planes[:].bitcast(I32), 0)
+        nc.vector.tensor_copy(bytes_got[:, 0:N], ks_pool[:].indirect(offsets[:]))
+        nc.vector.tensor_copy(bytes_got[:, N : 2 * N], cs_pool[:].indirect(offsets[:]))
         for quad in range(4):
             nc.sync.dma_start(
                 planes[32 * quad : 32 * quad + 4, :].bitcast(I32),
-                planes[top + 4 * quad : top + 4 * quad + 4, :].bitcast(I32),
+                bytes_got[top + 4 * quad : top + 4 * quad + 4, :].bitcast(I32),
             )
 
         hi = keep.tile([P, NQ * PACK], BF16, name="hi", align_bytes=64)
         lo = keep.tile([P, NQ * PACK], BF16, name="lo", align_bytes=64)
         q_walk = q_raw[:].rearrange("p (t c i) -> p c t i", t=PACK, i=4)
         nc.scalar.activation(hi[:].rearrange("p (c i t) -> p c t i", t=PACK, i=4), q_walk, relu)
-        neg = keep.tile([P, NQ * PACK], F32, name="neg", align_bytes=64)
-        nc.scalar.activation(neg[:].rearrange("p (c i t) -> p c t i", t=PACK, i=4), q_walk, relu, scale=-1.0)
-        nc.scalar.mul(lo[:], neg[:], -1.0)
+        lo_walk = lo[:].rearrange("p (c i t) -> p c t i", t=PACK, i=4)
+        cut = 32
+        nc.vector.tensor_scalar_min(lo_walk[:, 0:cut], q_walk[:, 0:cut], 0.0)
+        neg = keep.tile([P, (NQ // 4 - cut) * 16], F32, name="neg", align_bytes=64)
+        nc.scalar.activation(neg[:].rearrange("p (c i t) -> p c t i", t=PACK, i=4), q_walk[:, cut:], relu, scale=-1.0)
+        nc.scalar.mul(lo[:, cut * 16 :], neg[:], -1.0)
 
         kw_got = keep.tile([P, N], U32, name="kw_got", align_bytes=64)
         cw_got = keep.tile([P, N], U32, name="cw_got", align_bytes=64)
@@ -80,34 +81,35 @@ def tile_attend_quest_topk_kernel(tc, qT, k_words, k_scales, c_words, c_scales, 
             for tile in range(2):
                 banks[half, tile] = psum.tile([P, HALF], F32, name="bank%d%d" % (half, tile))
 
-        def passes(table, half, codes, scales, words):
+        def one_pass(table, half, tile):
+            codes, scales, words = ((hi_codes, hi_scales, kw_got), (lo_codes, lo_scales, cw_got))[table]
             first = table * N + half * HALF
-            for tile in range(2):
-                rows = slice(tile * P, (tile + 1) * P)
-                nc.tensor.matmul_mx(
-                    out=banks[half, tile][:],
-                    lhsT=codes[:, rows].bitcast(FP8X4),
-                    lhsT_scale=scales[:, rows],
-                    rhs=words[:, half * HALF : (half + 1) * HALF].bitcast(FP8X4),
-                    rhs_scale=planes[:, first : first + HALF],
-                    start=(table == 0),
-                    stop=(table == 1),
-                )
+            rows = slice(tile * P, (tile + 1) * P)
+            nc.tensor.matmul_mx(
+                out=banks[half, tile][:],
+                lhsT=codes[:, rows].bitcast(FP8X4),
+                lhsT_scale=scales[:, rows],
+                rhs=words[:, half * HALF : (half + 1) * HALF].bitcast(FP8X4),
+                rhs_scale=planes[:, first : first + HALF],
+                start=(table == 0),
+                stop=(table == 1),
+            )
 
-        for half in range(2):
-            passes(0, half, hi_codes, hi_scales, kw_got)
         for half in range(2):
             part = offsets[:, half * LIST_COLS // 2 : (half + 1) * LIST_COLS // 2]
             nc.vector.tensor_copy(cw_got[:, half * HALF : (half + 1) * HALF], cw_pool[:].bitcast(U32).indirect(part))
-            passes(1, half, lo_codes, lo_scales, cw_got)
-
-        early = keep.tile([P, 2, HALF], F32, name="early")
+        for table in range(2):
+            for tile in range(2):
+                one_pass(table, 0, tile)
         for tile in range(2):
-            nc.scalar.copy(early[:, tile, :], banks[0, tile][:])
-        nc.sync.dma_start(out[0].rearrange("(t p) n -> p t n", p=P)[:, :, 0:HALF], early[:])
-        late0 = keep.tile([P, HALF], F32, name="late0")
-        nc.vector.tensor_copy(late0[:], banks[1, 0][:])
-        nc.sync.dma_start(out[0, 0:P, HALF:N], late0[:])
-        late1 = keep.tile([P, HALF], F32, name="late1")
-        nc.scalar.copy(late1[:], banks[1, 1][:])
-        nc.scalar.dma_start(out[0, P:NQ, HALF:N], late1[:])
+            for table in range(2):
+                one_pass(table, 1, tile)
+
+        for half in range(2):
+            for tile in range(2):
+                result = keep.tile([P, HALF], F32, name="result%d%d" % (half, tile))
+                if half == 0:
+                    nc.scalar.copy(result[:], banks[half, tile][:])
+                else:
+                    nc.vector.tensor_copy(result[:], banks[half, tile][:])
+                nc.sync.dma_start(out[0, tile * P : (tile + 1) * P, half * HALF : (half + 1) * HALF], result[:])

@@ -76,40 +76,55 @@ def tile_attend_quest_topk_kernel(tc, qT, k_words, k_scales, c_words, c_scales, 
         nc.vector.tensor_copy(kw_got[:], kw_pool[:].bitcast(U32).indirect(offsets[:]))
         nc.vector.quantize_mx(out=lo_codes[:].bitcast(FP8X4), scales=lo_scales[:], in_=lo[:])
 
-        banks = {}
-        for half in range(2):
-            for tile in range(2):
-                banks[half, tile] = psum.tile([P, HALF], F32, name="bank%d%d" % (half, tile))
+        parts = [(0, 0, HALF), (1, 0, HALF), (0, HALF, HALF), (1, HALF, P), (1, HALF + P, P)]
+        banks = [psum.tile([P, width], F32, name="bank%d" % b) for b, (tile, first, width) in enumerate(parts)]
 
-        def one_pass(table, half, tile):
+        def one_pass(table, b):
             codes, scales, words = ((hi_codes, hi_scales, kw_got), (lo_codes, lo_scales, cw_got))[table]
-            first = table * N + half * HALF
+            tile, first, width = parts[b]
             rows = slice(tile * P, (tile + 1) * P)
             nc.tensor.matmul_mx(
-                out=banks[half, tile][:],
+                out=banks[b][:],
                 lhsT=codes[:, rows].bitcast(FP8X4),
                 lhsT_scale=scales[:, rows],
-                rhs=words[:, half * HALF : (half + 1) * HALF].bitcast(FP8X4),
-                rhs_scale=planes[:, first : first + HALF],
+                rhs=words[:, first : first + width].bitcast(FP8X4),
+                rhs_scale=planes[:, table * N + first : table * N + first + width],
                 start=(table == 0),
                 stop=(table == 1),
             )
+
+        warm = psum.tile([P, N], F32, name="warm")
+        nc.tensor.matmul_mx(
+            out=warm[:],
+            lhsT=lo_codes[:, 0:P].bitcast(FP8X4),
+            lhsT_scale=lo_scales[:, 0:P],
+            rhs=kw_got[:].bitcast(FP8X4),
+            rhs_scale=bytes_got[:, 0:N],
+            start=True,
+            stop=True,
+        )
 
         for half in range(2):
             part = offsets[:, half * LIST_COLS // 2 : (half + 1) * LIST_COLS // 2]
             nc.vector.tensor_copy(cw_got[:, half * HALF : (half + 1) * HALF], cw_pool[:].bitcast(U32).indirect(part))
         for table in range(2):
-            for tile in range(2):
-                one_pass(table, 0, tile)
-        for tile in range(2):
-            for table in range(2):
-                one_pass(table, 1, tile)
+            for b in range(2):
+                one_pass(table, b)
+        for table in range(2):
+            one_pass(table, 2)
+        for table in range(2):
+            for b in (3, 4):
+                one_pass(table, b)
 
-        for half in range(2):
-            for tile in range(2):
-                result = keep.tile([P, HALF], F32, name="result%d%d" % (half, tile))
-                if half == 0:
-                    nc.scalar.copy(result[:], banks[half, tile][:])
-                else:
-                    nc.vector.tensor_copy(result[:], banks[half, tile][:])
-                nc.sync.dma_start(out[0, tile * P : (tile + 1) * P, half * HALF : (half + 1) * HALF], result[:])
+        for b in range(3):
+            tile, first, width = parts[b]
+            result = keep.tile([P, HALF], F32, name="result%d" % b)
+            if b < 2:
+                nc.scalar.copy(result[:], banks[b][:])
+            else:
+                nc.vector.tensor_copy(result[:], banks[b][:])
+            nc.sync.dma_start(out[0, tile * P : (tile + 1) * P, first : first + width], result[:])
+        last = keep.tile([P, HALF], F32, name="last")
+        nc.scalar.copy(last[:, 0:P], banks[3][:])
+        nc.vector.tensor_copy(last[:, P:HALF], banks[4][:])
+        nc.sync.dma_start(out[0, P : 2 * P, HALF:N], last[:])

@@ -38,7 +38,10 @@ def tile_attend_quest_topk_kernel(tc, qT, k_words, k_scales, c_words, c_scales, 
         nc.scalar.dma_start(ks_pool[top:P, :].bitcast(I32), k_scales[0].bitcast(I32))
         nc.sync.dma_start(offsets[:], offs)
         nc.sync.dma_start(cs_pool[top:P, :].bitcast(I32), c_scales[0].bitcast(I32))
-        nc.sync.dma_start(q_raw[:], qT[0].rearrange("(p j) w -> p (j w)", j=PACK))
+        lead = 2 * NQ
+        q_rows = qT[0].rearrange("(p j) w -> p (j w)", j=PACK)
+        nc.sync.dma_start(q_raw[:, 0:lead], q_rows[:, 0:lead])
+        nc.sync.dma_start(q_raw[:, lead:], q_rows[:, lead:])
         nc.sync.dma_start(kw_pool[:], k_words[0].rearrange("p t r -> p (t r)").bitcast(I32))
         nc.sync.dma_start(cw_pool[:], c_words[0].rearrange("p t r -> p (t r)").bitcast(I32))
         nc.vector.memset(ks_pool[0:top, :].bitcast(I32), 0)
@@ -58,13 +61,12 @@ def tile_attend_quest_topk_kernel(tc, qT, k_words, k_scales, c_words, c_scales, 
         hi = keep.tile([P, NQ * PACK], BF16, name="hi", align_bytes=64)
         lo = keep.tile([P, NQ * PACK], BF16, name="lo", align_bytes=64)
         q_walk = q_raw[:].rearrange("p (t c i) -> p c t i", t=PACK, i=4)
+        neg = keep.tile([P, PACK * NQ], F32, name="neg", align_bytes=64)
+        nc.scalar.activation(neg[:, 0:lead], q_raw[:, 0:lead], relu, scale=-1.0)
         nc.scalar.activation(hi[:].rearrange("p (c i t) -> p c t i", t=PACK, i=4), q_walk, relu)
-        lo_walk = lo[:].rearrange("p (c i t) -> p c t i", t=PACK, i=4)
-        cut = 32
-        nc.vector.tensor_scalar_min(lo_walk[:, 0:cut], q_walk[:, 0:cut], 0.0)
-        neg = keep.tile([P, (NQ // 4 - cut) * 16], F32, name="neg", align_bytes=64)
-        nc.scalar.activation(neg[:].rearrange("p (c i t) -> p c t i", t=PACK, i=4), q_walk[:, cut:], relu, scale=-1.0)
-        nc.scalar.mul(lo[:, cut * 16 :], neg[:], -1.0)
+        nc.scalar.activation(neg[:, lead:], q_raw[:, lead:], relu, scale=-1.0)
+        neg_walk = neg[:].rearrange("p (t c i) -> p c t i", t=PACK, i=4)
+        nc.scalar.mul(lo[:].rearrange("p (c i t) -> p c t i", t=PACK, i=4), neg_walk, -1.0)
 
         kw_got = keep.tile([P, N], U32, name="kw_got", align_bytes=64)
         cw_got = keep.tile([P, N], U32, name="cw_got", align_bytes=64)

@@ -78,7 +78,7 @@ def tile_attend_quest_topk_kernel(tc, qT, k_words, k_scales, c_words, c_scales, 
         nc.vector.tensor_copy(kw_got[:], kw_pool[:].bitcast(U32).indirect(offsets[:]))
         nc.vector.quantize_mx(out=lo_codes[:].bitcast(FP8X4), scales=lo_scales[:], in_=lo[:])
 
-        parts = [(0, 0, HALF), (1, 0, HALF), (0, HALF, HALF), (1, HALF, P), (1, HALF + P, P)]
+        parts = [(0, 0, HALF), (1, 0, HALF), (0, HALF, P), (0, HALF + P, P), (1, HALF, P), (1, HALF + P, P)]
         banks = [psum.tile([P, width], F32, name="bank%d" % b) for b, (tile, first, width) in enumerate(parts)]
 
         def one_pass(table, b):
@@ -109,24 +109,17 @@ def tile_attend_quest_topk_kernel(tc, qT, k_words, k_scales, c_words, c_scales, 
         for half in range(2):
             part = offsets[:, half * LIST_COLS // 2 : (half + 1) * LIST_COLS // 2]
             nc.vector.tensor_copy(cw_got[:, half * HALF : (half + 1) * HALF], cw_pool[:].bitcast(U32).indirect(part))
-        for table in range(2):
-            for b in range(2):
-                one_pass(table, b)
-        for table in range(2):
-            one_pass(table, 2)
-        for table in range(2):
-            for b in (3, 4):
-                one_pass(table, b)
+        for pair in range(3):
+            for table in range(2):
+                for b in (2 * pair, 2 * pair + 1):
+                    one_pass(table, b)
 
-        for b in range(3):
-            tile, first, width = parts[b]
-            result = keep.tile([P, HALF], F32, name="result%d" % b)
-            if b < 2:
-                nc.scalar.copy(result[:], banks[b][:])
-            else:
-                nc.vector.tensor_copy(result[:], banks[b][:])
-            nc.sync.dma_start(out[0, tile * P : (tile + 1) * P, first : first + width], result[:])
-        last = keep.tile([P, HALF], F32, name="last")
-        nc.scalar.copy(last[:, 0:P], banks[3][:])
-        nc.vector.tensor_copy(last[:, P:HALF], banks[4][:])
-        nc.sync.dma_start(out[0, P : 2 * P, HALF:N], last[:])
+        for b in range(2):
+            result = keep.tile([P, HALF], F32, name="first%d" % b)
+            nc.scalar.copy(result[:], banks[b][:])
+            nc.sync.dma_start(out[0, b * P : (b + 1) * P, 0:HALF], result[:])
+        for tile in range(2):
+            result = keep.tile([P, HALF], F32, name="second%d" % tile)
+            nc.scalar.copy(result[:, 0:P], banks[2 + 2 * tile][:])
+            nc.vector.tensor_copy(result[:, P:HALF], banks[3 + 2 * tile][:])
+            nc.sync.dma_start(out[0, tile * P : (tile + 1) * P, HALF:N], result[:])

@@ -70,25 +70,23 @@ def tile_attend_quest_topk_kernel(tc, qT, k_words, k_scales, c_words, c_scales, 
 
         kw_got = keep.tile([P, N], U32, name="kw_got", align_bytes=64)
         cw_got = keep.tile([P, N], U32, name="cw_got", align_bytes=64)
-        hi_codes = keep.tile([P, NQ], U32, name="hi_codes", align_bytes=64)
-        lo_codes = keep.tile([P, NQ], U32, name="lo_codes", align_bytes=64)
-        hi_scales = keep.tile([P, NQ], U8, name="hi_scales", align_bytes=64)
-        lo_scales = keep.tile([P, NQ], U8, name="lo_scales", align_bytes=64)
-        nc.vector.quantize_mx(out=hi_codes[:].bitcast(FP8X4), scales=hi_scales[:], in_=hi[:])
+        q_codes = keep.tile([P, 2 * NQ], U32, name="q_codes", align_bytes=64)
+        q_scales = keep.tile([P, 2 * NQ], U8, name="q_scales", align_bytes=64)
+        nc.vector.quantize_mx(out=q_codes[:, 0:NQ].bitcast(FP8X4), scales=q_scales[:, 0:NQ], in_=hi[:])
         nc.vector.tensor_copy(kw_got[:], kw_pool[:].bitcast(U32).indirect(offsets[:]))
-        nc.vector.quantize_mx(out=lo_codes[:].bitcast(FP8X4), scales=lo_scales[:], in_=lo[:])
+        nc.vector.quantize_mx(out=q_codes[:, NQ:].bitcast(FP8X4), scales=q_scales[:, NQ:], in_=lo[:])
 
         parts = [(0, 0, HALF), (1, 0, HALF), (0, HALF, P), (0, HALF + P, P), (1, HALF, P), (1, HALF + P, P)]
         banks = [psum.tile([P, width], F32, name="bank%d" % b) for b, (tile, first, width) in enumerate(parts)]
 
         def one_pass(table, b):
-            codes, scales, words = ((hi_codes, hi_scales, kw_got), (lo_codes, lo_scales, cw_got))[table]
+            words = (kw_got, cw_got)[table]
             tile, first, width = parts[b]
-            rows = slice(tile * P, (tile + 1) * P)
+            rows = slice(table * NQ + tile * P, table * NQ + (tile + 1) * P)
             nc.tensor.matmul_mx(
                 out=banks[b][:],
-                lhsT=codes[:, rows].bitcast(FP8X4),
-                lhsT_scale=scales[:, rows],
+                lhsT=q_codes[:, rows].bitcast(FP8X4),
+                lhsT_scale=q_scales[:, rows],
                 rhs=words[:, first : first + width].bitcast(FP8X4),
                 rhs_scale=planes[:, table * N + first : table * N + first + width],
                 start=(table == 0),
@@ -98,10 +96,10 @@ def tile_attend_quest_topk_kernel(tc, qT, k_words, k_scales, c_words, c_scales, 
         warm = psum.tile([P, N], F32, name="warm")
         nc.tensor.matmul_mx(
             out=warm[:],
-            lhsT=lo_codes[:, 0:P].bitcast(FP8X4),
-            lhsT_scale=lo_scales[:, 0:P],
-            rhs=kw_got[:].bitcast(FP8X4),
-            rhs_scale=bytes_got[:, 0:N],
+            lhsT=q_codes[:, 0:P].bitcast(FP8X4),
+            lhsT_scale=q_scales[:, 0:P],
+            rhs=q_codes[:].bitcast(FP8X4),
+            rhs_scale=q_scales[:],
             start=True,
             stop=True,
         )

@@ -96,9 +96,9 @@ def tile_attend_quest_topk_kernel(tc, qT, k_words, k_scales, c_words, c_scales, 
         warm = psum.tile([P, N], F32, name="warm")
         nc.tensor.matmul_mx(
             out=warm[:],
-            lhsT=q_codes[:, 0:P].bitcast(FP8X4),
-            lhsT_scale=q_scales[:, 0:P],
-            rhs=q_codes[:].bitcast(FP8X4),
+            lhsT=q_codes[:, NQ : NQ + P].bitcast(FP8X4),
+            lhsT_scale=q_scales[:, NQ : NQ + P],
+            rhs=kw_got[:].bitcast(FP8X4),
             rhs_scale=q_scales[:],
             start=True,
             stop=True,

@@ -38,10 +38,7 @@ def tile_attend_quest_topk_kernel(tc, qT, k_words, k_scales, c_words, c_scales, 
         nc.scalar.dma_start(ks_pool[top:P, :].bitcast(I32), k_scales[0].bitcast(I32))
         nc.sync.dma_start(offsets[:], offs)
         nc.sync.dma_start(cs_pool[top:P, :].bitcast(I32), c_scales[0].bitcast(I32))
-        lead = 2 * NQ
-        q_rows = qT[0].rearrange("(p j) w -> p (j w)", j=PACK)
-        nc.sync.dma_start(q_raw[:, 0:lead], q_rows[:, 0:lead])
-        nc.sync.dma_start(q_raw[:, lead:], q_rows[:, lead:])
+        nc.sync.dma_start(q_raw[:], qT[0].rearrange("(p j) w -> p (j w)", j=PACK))
         nc.sync.dma_start(kw_pool[:], k_words[0].rearrange("p t r -> p (t r)").bitcast(I32))
         nc.sync.dma_start(cw_pool[:], c_words[0].rearrange("p t r -> p (t r)").bitcast(I32))
         nc.vector.memset(ks_pool[0:top, :].bitcast(I32), 0)
@@ -61,12 +58,13 @@ def tile_attend_quest_topk_kernel(tc, qT, k_words, k_scales, c_words, c_scales, 
         hi = keep.tile([P, NQ * PACK], BF16, name="hi", align_bytes=64)
         lo = keep.tile([P, NQ * PACK], BF16, name="lo", align_bytes=64)
         q_walk = q_raw[:].rearrange("p (t c i) -> p c t i", t=PACK, i=4)
-        neg = keep.tile([P, PACK * NQ], F32, name="neg", align_bytes=64)
-        nc.scalar.activation(neg[:, 0:lead], q_raw[:, 0:lead], relu, scale=-1.0)
         nc.scalar.activation(hi[:].rearrange("p (c i t) -> p c t i", t=PACK, i=4), q_walk, relu)
-        nc.scalar.activation(neg[:, lead:], q_raw[:, lead:], relu, scale=-1.0)
-        neg_walk = neg[:].rearrange("p (t c i) -> p c t i", t=PACK, i=4)
-        nc.scalar.mul(lo[:].rearrange("p (c i t) -> p c t i", t=PACK, i=4), neg_walk, -1.0)
+        lo_walk = lo[:].rearrange("p (c i t) -> p c t i", t=PACK, i=4)
+        cut = 32
+        nc.vector.tensor_scalar_min(lo_walk[:, 0:cut], q_walk[:, 0:cut], 0.0)
+        neg = keep.tile([P, (NQ // 4 - cut) * 16], F32, name="neg", align_bytes=64)
+        nc.scalar.activation(neg[:].rearrange("p (c i t) -> p c t i", t=PACK, i=4), q_walk[:, cut:], relu, scale=-1.0)
+        nc.scalar.mul(lo[:, cut * 16 :], neg[:], -1.0)
 
         kw_got = keep.tile([P, N], U32, name="kw_got", align_bytes=64)
         cw_got = keep.tile([P, N], U32, name="cw_got", align_bytes=64)

@@ -49,10 +49,10 @@ def tile_attend_quest_topk_kernel(tc, qT, k_words, k_scales, c_words, c_scales, 
         nc.vector.memset(planes[:].bitcast(I32), 0)
         nc.vector.tensor_copy(bytes_got[:, 0:N], ks_pool[:].indirect(offsets[:]))
         nc.vector.tensor_copy(bytes_got[:, N : 2 * N], cs_pool[:].indirect(offsets[:]))
-        for quad in range(4):
+        for row in range(4):
             nc.sync.dma_start(
-                planes[32 * quad : 32 * quad + 4, :].bitcast(I32),
-                bytes_got[top + 4 * quad : top + 4 * quad + 4, :].bitcast(I32),
+                planes[row:P:32, :].bitcast(I32),
+                bytes_got[top + row : P : 4, :].bitcast(I32),
             )
 
         hi = keep.tile([P, NQ * PACK], BF16, name="hi", align_bytes=64)
@@ -74,7 +74,7 @@ def tile_attend_quest_topk_kernel(tc, qT, k_words, k_scales, c_words, c_scales, 
         nc.vector.tensor_copy(kw_got[:], kw_pool[:].bitcast(U32).indirect(offsets[:]))
         nc.vector.quantize_mx(out=q_codes[:, NQ:].bitcast(FP8X4), scales=q_scales[:, NQ:], in_=lo[:])
 
-        parts = [(0, 0, HALF), (1, 0, HALF), (0, HALF, P), (0, HALF + P, P), (1, HALF, P), (1, HALF + P, P)]
+        parts = [(0, 0, P), (0, P, P), (1, 0, HALF), (0, HALF, P), (0, HALF + P, P), (1, HALF, P), (1, HALF + P, P)]
         banks = [psum.tile([P, width], F32, name="bank%d" % b) for b, (tile, first, width) in enumerate(parts)]
 
         def one_pass(table, b):
@@ -105,17 +105,18 @@ def tile_attend_quest_topk_kernel(tc, qT, k_words, k_scales, c_words, c_scales, 
         for half in range(2):
             part = offsets[:, half * LIST_COLS // 2 : (half + 1) * LIST_COLS // 2]
             nc.vector.tensor_copy(cw_got[:, half * HALF : (half + 1) * HALF], cw_pool[:].bitcast(U32).indirect(part))
-        for pair in range(3):
+        for group in ((0, 1, 2), (3, 4), (5, 6)):
             for table in range(2):
-                for b in (2 * pair, 2 * pair + 1):
+                for b in group:
                     one_pass(table, b)
 
-        for b in range(2):
-            result = keep.tile([P, HALF], F32, name="first%d" % b)
-            nc.scalar.copy(result[:], banks[b][:])
-            nc.sync.dma_start(out[0, b * P : (b + 1) * P, 0:HALF], result[:])
+        for tile, group in enumerate(((0, 1), (2,))):
+            result = keep.tile([P, HALF], F32, name="first%d" % tile)
+            for b in group:
+                nc.scalar.copy(result[:, parts[b][1] : parts[b][1] + parts[b][2]], banks[b][:])
+            nc.sync.dma_start(out[0, tile * P : (tile + 1) * P, 0:HALF], result[:])
         for tile in range(2):
             result = keep.tile([P, HALF], F32, name="second%d" % tile)
-            nc.scalar.copy(result[:, 0:P], banks[2 + 2 * tile][:])
-            nc.vector.tensor_copy(result[:, P:HALF], banks[3 + 2 * tile][:])
+            nc.scalar.copy(result[:, 0:P], banks[3 + 2 * tile][:])
+            nc.vector.tensor_copy(result[:, P:HALF], banks[4 + 2 * tile][:])
             nc.sync.dma_start(out[0, tile * P : (tile + 1) * P, HALF:N], result[:])

@@ -34,15 +34,19 @@ def tile_attend_quest_topk_kernel(tc, qT, k_words, k_scales, c_words, c_scales, 
         kw_pool = keep.tile([P, T], I32, name="kw_pool", align_bytes=64)
         cw_pool = keep.tile([P, T], I32, name="cw_pool", align_bytes=64)
 
-        top = P - ROWS
-        nc.scalar.dma_start(ks_pool[top:P, :].bitcast(I32), k_scales[0].bitcast(I32))
+        first_row, step = 32, 4
+        live = slice(first_row, first_row + step * ROWS, step)
+        k_rows = k_words[0].rearrange("p t r -> p (t r)").bitcast(I32)
+        lead = T // 4
+        nc.vector.memset(ks_pool[:].bitcast(I32), 0)
+        nc.vector.memset(cs_pool[:].bitcast(I32), 0)
+        nc.sync.dma_start(kw_pool[:, 0:lead], k_rows[:, 0:lead])
         nc.sync.dma_start(offsets[:], offs)
-        nc.sync.dma_start(cs_pool[top:P, :].bitcast(I32), c_scales[0].bitcast(I32))
+        nc.sync.dma_start(ks_pool[live, :].bitcast(I32), k_scales[0].bitcast(I32))
         nc.sync.dma_start(q_raw[:], qT[0].rearrange("(p j) w -> p (j w)", j=PACK))
-        nc.sync.dma_start(kw_pool[:], k_words[0].rearrange("p t r -> p (t r)").bitcast(I32))
+        nc.sync.dma_start(cs_pool[live, :].bitcast(I32), c_scales[0].bitcast(I32))
+        nc.sync.dma_start(kw_pool[:, lead:], k_rows[:, lead:])
         nc.sync.dma_start(cw_pool[:], c_words[0].rearrange("p t r -> p (t r)").bitcast(I32))
-        nc.vector.memset(ks_pool[0:top, :].bitcast(I32), 0)
-        nc.vector.memset(cs_pool[0:top, :].bitcast(I32), 0)
 
         bytes_got = keep.tile([P, 2 * N], U8, name="bytes_got", align_bytes=64)
         planes = keep.tile([P, 2 * N], U8, name="planes", align_bytes=64)
@@ -50,9 +54,10 @@ def tile_attend_quest_topk_kernel(tc, qT, k_words, k_scales, c_words, c_scales, 
         nc.vector.tensor_copy(bytes_got[:, 0:N], ks_pool[:].indirect(offsets[:]))
         nc.vector.tensor_copy(bytes_got[:, N : 2 * N], cs_pool[:].indirect(offsets[:]))
         for row in range(4):
+            source = first_row + step * row
             nc.sync.dma_start(
                 planes[row:P:32, :].bitcast(I32),
-                bytes_got[top + row : P : 4, :].bitcast(I32),
+                bytes_got[source : source + 4 * 4 * step : 4 * step, :].bitcast(I32),
             )
 
         hi = keep.tile([P, NQ * PACK], BF16, name="hi", align_bytes=64)

@@ -36,16 +36,13 @@ def tile_attend_quest_topk_kernel(tc, qT, k_words, k_scales, c_words, c_scales, 
 
         first_row, step = 32, 4
         live = slice(first_row, first_row + step * ROWS, step)
-        k_rows = k_words[0].rearrange("p t r -> p (t r)").bitcast(I32)
-        lead = T // 4
         nc.vector.memset(ks_pool[:].bitcast(I32), 0)
         nc.vector.memset(cs_pool[:].bitcast(I32), 0)
-        nc.sync.dma_start(kw_pool[:, 0:lead], k_rows[:, 0:lead])
+        nc.sync.dma_start(q_raw[:], qT[0].rearrange("(p j) w -> p (j w)", j=PACK))
         nc.sync.dma_start(offsets[:], offs)
         nc.sync.dma_start(ks_pool[live, :].bitcast(I32), k_scales[0].bitcast(I32))
-        nc.sync.dma_start(q_raw[:], qT[0].rearrange("(p j) w -> p (j w)", j=PACK))
         nc.sync.dma_start(cs_pool[live, :].bitcast(I32), c_scales[0].bitcast(I32))
-        nc.sync.dma_start(kw_pool[:, lead:], k_rows[:, lead:])
+        nc.sync.dma_start(kw_pool[:], k_words[0].rearrange("p t r -> p (t r)").bitcast(I32))
         nc.sync.dma_start(cw_pool[:], c_words[0].rearrange("p t r -> p (t r)").bitcast(I32))
 
         bytes_got = keep.tile([P, 2 * N], U8, name="bytes_got", align_bytes=64)
@@ -65,7 +62,7 @@ def tile_attend_quest_topk_kernel(tc, qT, k_words, k_scales, c_words, c_scales, 
         q_walk = q_raw[:].rearrange("p (t c i) -> p c t i", t=PACK, i=4)
         nc.scalar.activation(hi[:].rearrange("p (c i t) -> p c t i", t=PACK, i=4), q_walk, relu)
         lo_walk = lo[:].rearrange("p (c i t) -> p c t i", t=PACK, i=4)
-        cut = 32
+        cut = 16
         nc.vector.tensor_scalar_min(lo_walk[:, 0:cut], q_walk[:, 0:cut], 0.0)
         neg = keep.tile([P, (NQ // 4 - cut) * 16], F32, name="neg", align_bytes=64)
         nc.scalar.activation(neg[:].rearrange("p (c i t) -> p c t i", t=PACK, i=4), q_walk[:, cut:], relu, scale=-1.0)

@@ -18,6 +18,7 @@ PACK = 4
 ROWS = 16
 HALF = N // 2
 LIST_COLS = N // 16
+WARM_ROWS = 32
 
 
 def tile_attend_quest_topk_kernel(tc, qT, k_words, k_scales, c_words, c_scales, offs, out):
@@ -64,49 +65,55 @@ def tile_attend_quest_topk_kernel(tc, qT, k_words, k_scales, c_words, c_scales, 
         lo_walk = lo[:].rearrange("p (c i t) -> p c t i", t=PACK, i=4)
         cut = 16
         nc.vector.tensor_scalar_min(lo_walk[:, 0:cut], q_walk[:, 0:cut], 0.0)
-        neg = keep.tile([P, (NQ // 4 - cut) * 16], F32, name="neg", align_bytes=64)
+        neg = keep.tile([P, (NQ // 4 - cut) * 16], F32, name="neg", tag="neg", align_bytes=64)
         nc.scalar.activation(neg[:].rearrange("p (c i t) -> p c t i", t=PACK, i=4), q_walk[:, cut:], relu, scale=-1.0)
         nc.scalar.mul(lo[:, cut * 16 :], neg[:], -1.0)
 
-        kw_got = keep.tile([P, N], U32, name="kw_got", align_bytes=64)
+        kw_first = keep.tile([P, HALF], U32, name="kw_first", align_bytes=64)
         cw_got = keep.tile([P, N], U32, name="cw_got", align_bytes=64)
         q_codes = keep.tile([P, 2 * NQ], U32, name="q_codes", align_bytes=64)
         q_scales = keep.tile([P, 2 * NQ], U8, name="q_scales", align_bytes=64)
         nc.vector.quantize_mx(out=q_codes[:, 0:NQ].bitcast(FP8X4), scales=q_scales[:, 0:NQ], in_=hi[:])
-        nc.vector.tensor_copy(kw_got[:], kw_pool[:].bitcast(U32).indirect(offsets[:]))
+        halves = [offsets[:, half * LIST_COLS // 2 : (half + 1) * LIST_COLS // 2] for half in range(2)]
+        nc.vector.tensor_copy(kw_first[:], kw_pool[:].bitcast(U32).indirect(halves[0]))
         nc.vector.quantize_mx(out=q_codes[:, NQ:].bitcast(FP8X4), scales=q_scales[:, NQ:], in_=lo[:])
+        kw_second = keep.tile([P, HALF], U32, name="kw_second", tag="neg", align_bytes=64)
+        nc.vector.tensor_copy(kw_second[:], kw_pool[:].bitcast(U32).indirect(halves[1]))
 
         parts = [(0, 0, P), (0, P, P), (1, 0, HALF), (0, HALF, P), (0, HALF + P, P), (1, HALF, P), (1, HALF + P, P)]
         banks = [psum.tile([P, width], F32, name="bank%d" % b) for b, (tile, first, width) in enumerate(parts)]
 
         def one_pass(table, b):
-            words = (kw_got, cw_got)[table]
             tile, first, width = parts[b]
+            if table == 0:
+                words = (kw_first, kw_second)[first // HALF][:, first % HALF : first % HALF + width]
+            else:
+                words = cw_got[:, first : first + width]
             rows = slice(table * NQ + tile * P, table * NQ + (tile + 1) * P)
             nc.tensor.matmul_mx(
                 out=banks[b][:],
                 lhsT=q_codes[:, rows].bitcast(FP8X4),
                 lhsT_scale=q_scales[:, rows],
-                rhs=words[:, first : first + width].bitcast(FP8X4),
+                rhs=words.bitcast(FP8X4),
                 rhs_scale=planes[:, table * N + first : table * N + first + width],
                 start=(table == 0),
                 stop=(table == 1),
             )
 
-        warm = psum.tile([P, N], F32, name="warm")
-        nc.tensor.matmul_mx(
-            out=warm[:],
-            lhsT=q_codes[:, NQ : NQ + P].bitcast(FP8X4),
-            lhsT_scale=q_scales[:, NQ : NQ + P],
-            rhs=kw_got[:].bitcast(FP8X4),
-            rhs_scale=q_scales[:],
-            start=True,
-            stop=True,
-        )
+        warm = psum.tile([WARM_ROWS, N], F32, name="warm")
+        for first, width in ((0, N), (NQ, P), (NQ + P, P)):
+            nc.tensor.matmul_mx(
+                out=warm[:, 0:width],
+                lhsT=q_codes[:, NQ : NQ + WARM_ROWS].bitcast(FP8X4),
+                lhsT_scale=q_scales[:, NQ : NQ + WARM_ROWS],
+                rhs=q_codes[:, first : first + width].bitcast(FP8X4),
+                rhs_scale=q_scales[:, first : first + width],
+                start=True,
+                stop=True,
+            )
 
         for half in range(2):
-            part = offsets[:, half * LIST_COLS // 2 : (half + 1) * LIST_COLS // 2]
-            nc.vector.tensor_copy(cw_got[:, half * HALF : (half + 1) * HALF], cw_pool[:].bitcast(U32).indirect(part))
+            nc.vector.tensor_copy(cw_got[:, half * HALF : (half + 1) * HALF], cw_pool[:].bitcast(U32).indirect(halves[half]))
         for group in ((0, 1, 2), (3, 4), (5, 6)):
             for table in range(2):
                 for b in group:

@@ -31,12 +31,12 @@ def tile_attend_quest_topk_kernel(tc, qT, k_words, k_scales, c_words, c_scales, 
         offsets = keep.tile([P, LIST_COLS], U16, name="offsets")
         ks_pool = keep.tile([P, T], U8, name="ks_pool", align_bytes=64)
         cs_pool = keep.tile([P, T], U8, name="cs_pool", align_bytes=64)
-        q_raw = keep.tile([P, PACK * NQ], F32, name="q_raw", align_bytes=64)
+        q_raw = keep.tile([P, PACK * NQ], F32, name="q_raw", tag="q_raw", align_bytes=64)
         kw_pool = keep.tile([P, T], I32, name="kw_pool", align_bytes=64)
         cw_pool = keep.tile([P, T], I32, name="cw_pool", align_bytes=64)
 
-        first_row, step = 32, 4
-        live = slice(first_row, first_row + step * ROWS, step)
+        step = 8
+        live = slice(0, step * ROWS, step)
         nc.vector.memset(ks_pool[:].bitcast(I32), 0)
         nc.vector.memset(cs_pool[:].bitcast(I32), 0)
         nc.sync.dma_start(q_raw[:], qT[0].rearrange("(p j) w -> p (j w)", j=PACK))
@@ -47,37 +47,40 @@ def tile_attend_quest_topk_kernel(tc, qT, k_words, k_scales, c_words, c_scales, 
         nc.sync.dma_start(cw_pool[:], c_words[0].rearrange("p t r -> p (t r)").bitcast(I32))
 
         bytes_got = keep.tile([P, 2 * N], U8, name="bytes_got", align_bytes=64)
-        planes = keep.tile([P, 2 * N], U8, name="planes", align_bytes=64)
-        nc.vector.memset(planes[:].bitcast(I32), 0)
         nc.vector.tensor_copy(bytes_got[:, 0:N], ks_pool[:].indirect(offsets[:]))
         nc.vector.tensor_copy(bytes_got[:, N : 2 * N], cs_pool[:].indirect(offsets[:]))
-        for row in range(4):
-            source = first_row + step * row
-            nc.sync.dma_start(
-                planes[row:P:32, :].bitcast(I32),
-                bytes_got[source : source + 4 * 4 * step : 4 * step, :].bitcast(I32),
-            )
 
         hi = keep.tile([P, NQ * PACK], BF16, name="hi", align_bytes=64)
         lo = keep.tile([P, NQ * PACK], BF16, name="lo", align_bytes=64)
         q_walk = q_raw[:].rearrange("p (t c i) -> p c t i", t=PACK, i=4)
-        nc.scalar.activation(hi[:].rearrange("p (c i t) -> p c t i", t=PACK, i=4), q_walk, relu)
         lo_walk = lo[:].rearrange("p (c i t) -> p c t i", t=PACK, i=4)
         cut = 16
         nc.vector.tensor_scalar_min(lo_walk[:, 0:cut], q_walk[:, 0:cut], 0.0)
-        neg = keep.tile([P, (NQ // 4 - cut) * 16], F32, name="neg", tag="neg", align_bytes=64)
-        nc.scalar.activation(neg[:].rearrange("p (c i t) -> p c t i", t=PACK, i=4), q_walk[:, cut:], relu, scale=-1.0)
-        nc.scalar.mul(lo[:, cut * 16 :], neg[:], -1.0)
+        piece = (NQ // 4 - cut) // 2
+        negs = [keep.tile([P, piece * 16], F32, name="neg%d" % i, tag="neg%d" % i, align_bytes=64) for i in range(2)]
+        for i in range(2):
+            first = cut + i * piece
+            nc.scalar.activation(negs[i][:].rearrange("p (c i t) -> p c t i", t=PACK, i=4), q_walk[:, first : first + piece], relu, scale=-1.0)
+        for i in range(2):
+            first = cut + i * piece
+            nc.scalar.mul(lo[:, first * 16 : (first + piece) * 16], negs[i][:], -1.0)
+        nc.scalar.activation(hi[:].rearrange("p (c i t) -> p c t i", t=PACK, i=4), q_walk, relu)
+
+        q_codes = keep.tile([P, 2 * NQ], U32, name="q_codes", align_bytes=64)
+        q_scales = keep.tile([P, 2 * NQ], U8, name="q_scales", align_bytes=64)
+        nc.vector.quantize_mx(out=q_codes[:, NQ:].bitcast(FP8X4), scales=q_scales[:, NQ:], in_=lo[:])
+
+        planes = keep.tile([P, 2 * N], U8, name="planes", tag="neg1", align_bytes=64)
+        nc.vector.tensor_copy(planes[:].bitcast(I32), bytes_got[:].bitcast(I32))
+        for row in range(1, 4):
+            nc.sync.dma_start(planes[row:P:32, :].bitcast(I32), bytes_got[step * row : P : 32, :].bitcast(I32))
 
         kw_first = keep.tile([P, HALF], U32, name="kw_first", align_bytes=64)
         cw_got = keep.tile([P, N], U32, name="cw_got", align_bytes=64)
-        q_codes = keep.tile([P, 2 * NQ], U32, name="q_codes", align_bytes=64)
-        q_scales = keep.tile([P, 2 * NQ], U8, name="q_scales", align_bytes=64)
-        nc.vector.quantize_mx(out=q_codes[:, 0:NQ].bitcast(FP8X4), scales=q_scales[:, 0:NQ], in_=hi[:])
         halves = [offsets[:, half * LIST_COLS // 2 : (half + 1) * LIST_COLS // 2] for half in range(2)]
         nc.vector.tensor_copy(kw_first[:], kw_pool[:].bitcast(U32).indirect(halves[0]))
-        nc.vector.quantize_mx(out=q_codes[:, NQ:].bitcast(FP8X4), scales=q_scales[:, NQ:], in_=lo[:])
-        kw_second = keep.tile([P, HALF], U32, name="kw_second", tag="neg", align_bytes=64)
+        nc.vector.quantize_mx(out=q_codes[:, 0:NQ].bitcast(FP8X4), scales=q_scales[:, 0:NQ], in_=hi[:])
+        kw_second = keep.tile([P, HALF], U32, name="kw_second", tag="q_raw", align_bytes=64)
         nc.vector.tensor_copy(kw_second[:], kw_pool[:].bitcast(U32).indirect(halves[1]))
 
         parts = [(0, 0, P), (0, P, P), (1, 0, HALF), (0, HALF, P), (0, HALF + P, P), (1, HALF, P), (1, HALF + P, P)]
@@ -101,11 +104,11 @@ def tile_attend_quest_topk_kernel(tc, qT, k_words, k_scales, c_words, c_scales, 
             )
 
         warm = psum.tile([WARM_ROWS, N], F32, name="warm")
-        for first, width in ((0, N), (NQ, P), (NQ + P, P)):
+        for first, width in ((0, N), (0, P), (P, P)):
             nc.tensor.matmul_mx(
                 out=warm[:, 0:width],
-                lhsT=q_codes[:, NQ : NQ + WARM_ROWS].bitcast(FP8X4),
-                lhsT_scale=q_scales[:, NQ : NQ + WARM_ROWS],
+                lhsT=q_codes[:, 0:WARM_ROWS].bitcast(FP8X4),
+                lhsT_scale=q_scales[:, 0:WARM_ROWS],
                 rhs=q_codes[:, first : first + width].bitcast(FP8X4),
                 rhs_scale=q_scales[:, first : first + width],
                 start=True,

@@ -36,19 +36,24 @@ def tile_attend_quest_topk_kernel(tc, qT, k_words, k_scales, c_words, c_scales, 
         cw_pool = keep.tile([P, T], I32, name="cw_pool", align_bytes=64)
 
         step = 8
-        live = slice(0, step * ROWS, step)
+        c_first = 4
         nc.vector.memset(ks_pool[:].bitcast(I32), 0)
         nc.vector.memset(cs_pool[:].bitcast(I32), 0)
         nc.sync.dma_start(q_raw[:], qT[0].rearrange("(p j) w -> p (j w)", j=PACK))
         nc.sync.dma_start(offsets[:], offs)
-        nc.sync.dma_start(ks_pool[live, :].bitcast(I32), k_scales[0].bitcast(I32))
-        nc.sync.dma_start(cs_pool[live, :].bitcast(I32), c_scales[0].bitcast(I32))
+        nc.sync.dma_start(ks_pool[0:P:step, :].bitcast(I32), k_scales[0].bitcast(I32))
+        nc.sync.dma_start(cs_pool[c_first:P:step, :].bitcast(I32), c_scales[0].bitcast(I32))
         nc.sync.dma_start(kw_pool[:], k_words[0].rearrange("p t r -> p (t r)").bitcast(I32))
         nc.sync.dma_start(cw_pool[:], c_words[0].rearrange("p t r -> p (t r)").bitcast(I32))
 
         bytes_got = keep.tile([P, 2 * N], U8, name="bytes_got", align_bytes=64)
         nc.vector.tensor_copy(bytes_got[:, 0:N], ks_pool[:].indirect(offsets[:]))
         nc.vector.tensor_copy(bytes_got[:, N : 2 * N], cs_pool[:].indirect(offsets[:]))
+
+        def place_rows(plane, got, first):
+            nc.vector.tensor_copy(plane[:].bitcast(I32), got.bitcast(I32))
+            for row in range(1, 4):
+                nc.sync.dma_start(plane[first + row : P : 32, :].bitcast(I32), got[first + step * row : P : 32, :].bitcast(I32))
 
         hi = keep.tile([P, NQ * PACK], BF16, name="hi", align_bytes=64)
         lo = keep.tile([P, NQ * PACK], BF16, name="lo", align_bytes=64)
@@ -66,14 +71,15 @@ def tile_attend_quest_topk_kernel(tc, qT, k_words, k_scales, c_words, c_scales, 
             nc.scalar.mul(lo[:, first * 16 : (first + piece) * 16], negs[i][:], -1.0)
         nc.scalar.activation(hi[:].rearrange("p (c i t) -> p c t i", t=PACK, i=4), q_walk, relu)
 
+        k_plane = keep.tile([P, N], U8, name="k_plane", tag="neg0", align_bytes=64)
+        place_rows(k_plane, bytes_got[:, 0:N], 0)
+
         q_codes = keep.tile([P, 2 * NQ], U32, name="q_codes", align_bytes=64)
         q_scales = keep.tile([P, 2 * NQ], U8, name="q_scales", align_bytes=64)
         nc.vector.quantize_mx(out=q_codes[:, NQ:].bitcast(FP8X4), scales=q_scales[:, NQ:], in_=lo[:])
 
-        planes = keep.tile([P, 2 * N], U8, name="planes", tag="neg1", align_bytes=64)
-        nc.vector.tensor_copy(planes[:].bitcast(I32), bytes_got[:].bitcast(I32))
-        for row in range(1, 4):
-            nc.sync.dma_start(planes[row:P:32, :].bitcast(I32), bytes_got[step * row : P : 32, :].bitcast(I32))
+        c_plane = keep.tile([P, N], U8, name="c_plane", tag="neg1", align_bytes=64)
+        place_rows(c_plane, bytes_got[:, N : 2 * N], c_first)
 
         kw_first = keep.tile([P, HALF], U32, name="kw_first", align_bytes=64)
         cw_got = keep.tile([P, N], U32, name="cw_got", align_bytes=64)
@@ -86,7 +92,7 @@ def tile_attend_quest_topk_kernel(tc, qT, k_words, k_scales, c_words, c_scales, 
         parts = [(0, 0, P), (0, P, P), (1, 0, HALF), (0, HALF, P), (0, HALF + P, P), (1, HALF, P), (1, HALF + P, P)]
         banks = [psum.tile([P, width], F32, name="bank%d" % b) for b, (tile, first, width) in enumerate(parts)]
 
-        def one_pass(table, b):
+        def one_pass(table, b, opens):
             tile, first, width = parts[b]
             if table == 0:
                 words = (kw_first, kw_second)[first // HALF][:, first % HALF : first % HALF + width]
@@ -98,9 +104,9 @@ def tile_attend_quest_topk_kernel(tc, qT, k_words, k_scales, c_words, c_scales, 
                 lhsT=q_codes[:, rows].bitcast(FP8X4),
                 lhsT_scale=q_scales[:, rows],
                 rhs=words.bitcast(FP8X4),
-                rhs_scale=planes[:, table * N + first : table * N + first + width],
-                start=(table == 0),
-                stop=(table == 1),
+                rhs_scale=(k_plane[:], c_plane[c_first:P, :])[table][:, first : first + width],
+                start=opens,
+                stop=not opens,
             )
 
         warm = psum.tile([WARM_ROWS, N], F32, name="warm")
@@ -117,10 +123,15 @@ def tile_attend_quest_topk_kernel(tc, qT, k_words, k_scales, c_words, c_scales, 
 
         for half in range(2):
             nc.vector.tensor_copy(cw_got[:, half * HALF : (half + 1) * HALF], cw_pool[:].bitcast(U32).indirect(halves[half]))
-        for group in ((0, 1, 2), (3, 4), (5, 6)):
-            for table in range(2):
+        early = 4
+        for b in range(early):
+            one_pass(0, b, True)
+        for b in range(early):
+            one_pass(1, b, False)
+        for group in ((4,), (5, 6)):
+            for table in (1, 0):
                 for b in group:
-                    one_pass(table, b)
+                    one_pass(table, b, table == 1)
 
         for tile, group in enumerate(((0, 1), (2,))):
             result = keep.tile([P, HALF], F32, name="first%d" % tile)

@@ -121,17 +121,16 @@ def tile_attend_quest_topk_kernel(tc, qT, k_words, k_scales, c_words, c_scales, 
                 stop=True,
             )
 
-        for half in range(2):
-            nc.vector.tensor_copy(cw_got[:, half * HALF : (half + 1) * HALF], cw_pool[:].bitcast(U32).indirect(halves[half]))
-        early = 4
+        for first, last in ((0, HALF), (HALF, HALF + P), (HALF + P, N)):
+            nc.vector.tensor_copy(cw_got[:, first:last], cw_pool[:].bitcast(U32).indirect(offsets[:, first // 16 : last // 16]))
+        early = 3
         for b in range(early):
             one_pass(0, b, True)
         for b in range(early):
             one_pass(1, b, False)
-        for group in ((4,), (5, 6)):
-            for table in (1, 0):
-                for b in group:
-                    one_pass(table, b, table == 1)
+        for b in range(early, len(parts)):
+            one_pass(1, b, True)
+            one_pass(0, b, False)
 
         for tile, group in enumerate(((0, 1), (2,))):
             result = keep.tile([P, HALF], F32, name="first%d" % tile)

@@ -89,27 +89,7 @@ def tile_attend_quest_topk_kernel(tc, qT, k_words, k_scales, c_words, c_scales, 
         kw_second = keep.tile([P, HALF], U32, name="kw_second", tag="q_raw", align_bytes=64)
         nc.vector.tensor_copy(kw_second[:], kw_pool[:].bitcast(U32).indirect(halves[1]))
 
-        parts = [(0, 0, P), (0, P, P), (1, 0, HALF), (0, HALF, P), (0, HALF + P, P), (1, HALF, P), (1, HALF + P, P)]
-        banks = [psum.tile([P, width], F32, name="bank%d" % b) for b, (tile, first, width) in enumerate(parts)]
-
-        def one_pass(table, b, opens):
-            tile, first, width = parts[b]
-            if table == 0:
-                words = (kw_first, kw_second)[first // HALF][:, first % HALF : first % HALF + width]
-            else:
-                words = cw_got[:, first : first + width]
-            rows = slice(table * NQ + tile * P, table * NQ + (tile + 1) * P)
-            nc.tensor.matmul_mx(
-                out=banks[b][:],
-                lhsT=q_codes[:, rows].bitcast(FP8X4),
-                lhsT_scale=q_scales[:, rows],
-                rhs=words.bitcast(FP8X4),
-                rhs_scale=(k_plane[:], c_plane[c_first:P, :])[table][:, first : first + width],
-                start=opens,
-                stop=not opens,
-            )
-
-        warm = psum.tile([WARM_ROWS, N], F32, name="warm")
+        warm = psum.tile([WARM_ROWS, N], F32, name="warm", tag="bank7")
         for first, width in ((0, N), (0, P), (P, P)):
             nc.tensor.matmul_mx(
                 out=warm[:, 0:width],
@@ -121,9 +101,29 @@ def tile_attend_quest_topk_kernel(tc, qT, k_words, k_scales, c_words, c_scales, 
                 stop=True,
             )
 
-        for first, last in ((0, HALF), (HALF, HALF + P), (HALF + P, N)):
-            nc.vector.tensor_copy(cw_got[:, first:last], cw_pool[:].bitcast(U32).indirect(offsets[:, first // 16 : last // 16]))
-        early = 3
+        parts = [(tile, half * HALF + piece * P) for half in range(2) for tile in range(2) for piece in range(2)]
+        banks = [psum.tile([P, P], F32, name="bank%d" % b, tag="bank%d" % b) for b in range(len(parts))]
+
+        def one_pass(table, b, opens):
+            tile, first = parts[b]
+            if table == 0:
+                words = (kw_first, kw_second)[first // HALF][:, first % HALF : first % HALF + P]
+            else:
+                words = cw_got[:, first : first + P]
+            rows = slice(table * NQ + tile * P, table * NQ + (tile + 1) * P)
+            nc.tensor.matmul_mx(
+                out=banks[b][:],
+                lhsT=q_codes[:, rows].bitcast(FP8X4),
+                lhsT_scale=q_scales[:, rows],
+                rhs=words.bitcast(FP8X4),
+                rhs_scale=(k_plane[:], c_plane[c_first:P, :])[table][:, first : first + P],
+                start=opens,
+                stop=not opens,
+            )
+
+        for first in range(0, N, P):
+            nc.vector.tensor_copy(cw_got[:, first : first + P], cw_pool[:].bitcast(U32).indirect(offsets[:, first // 16 : (first + P) // 16]))
+        early = 4
         for b in range(early):
             one_pass(0, b, True)
         for b in range(early):
@@ -132,13 +132,12 @@ def tile_attend_quest_topk_kernel(tc, qT, k_words, k_scales, c_words, c_scales, 
             one_pass(1, b, True)
             one_pass(0, b, False)
 
-        for tile, group in enumerate(((0, 1), (2,))):
-            result = keep.tile([P, HALF], F32, name="first%d" % tile)
-            for b in group:
-                nc.scalar.copy(result[:, parts[b][1] : parts[b][1] + parts[b][2]], banks[b][:])
-            nc.sync.dma_start(out[0, tile * P : (tile + 1) * P, 0:HALF], result[:])
-        for tile in range(2):
-            result = keep.tile([P, HALF], F32, name="second%d" % tile)
-            nc.scalar.copy(result[:, 0:P], banks[3 + 2 * tile][:])
-            nc.vector.tensor_copy(result[:, P:HALF], banks[4 + 2 * tile][:])
-            nc.sync.dma_start(out[0, tile * P : (tile + 1) * P, HALF:N], result[:])
+        for store in range(4):
+            tile, first = parts[2 * store]
+            result = keep.tile([P, HALF], F32, name="result%d" % store)
+            for piece in range(2):
+                if store == 2:
+                    nc.vector.tensor_copy(result[:, piece * P : (piece + 1) * P], banks[2 * store + piece][:])
+                else:
+                    nc.scalar.copy(result[:, piece * P : (piece + 1) * P], banks[2 * store + piece][:])
+            nc.sync.dma_start(out[0, tile * P : (tile + 1) * P, first : first + HALF], result[:])

@@ -81,13 +81,12 @@ def tile_attend_quest_topk_kernel(tc, qT, k_words, k_scales, c_words, c_scales, 
         c_plane = keep.tile([P, N], U8, name="c_plane", tag="neg1", align_bytes=64)
         place_rows(c_plane, bytes_got[:, N : 2 * N], c_first)
 
-        kw_first = keep.tile([P, HALF], U32, name="kw_first", align_bytes=64)
+        kw_first = keep.tile([P, P], U32, name="kw_first", align_bytes=64)
         cw_got = keep.tile([P, N], U32, name="cw_got", align_bytes=64)
-        halves = [offsets[:, half * LIST_COLS // 2 : (half + 1) * LIST_COLS // 2] for half in range(2)]
-        nc.vector.tensor_copy(kw_first[:], kw_pool[:].bitcast(U32).indirect(halves[0]))
+        nc.vector.tensor_copy(kw_first[:], kw_pool[:].bitcast(U32).indirect(offsets[:, 0 : P // 16]))
         nc.vector.quantize_mx(out=q_codes[:, 0:NQ].bitcast(FP8X4), scales=q_scales[:, 0:NQ], in_=hi[:])
-        kw_second = keep.tile([P, HALF], U32, name="kw_second", tag="q_raw", align_bytes=64)
-        nc.vector.tensor_copy(kw_second[:], kw_pool[:].bitcast(U32).indirect(halves[1]))
+        kw_second = keep.tile([P, N - P], U32, name="kw_second", tag="q_raw", align_bytes=64)
+        nc.vector.tensor_copy(kw_second[:], kw_pool[:].bitcast(U32).indirect(offsets[:, P // 16 :]))
 
         warm = psum.tile([WARM_ROWS, N], F32, name="warm", tag="bank7")
         for first, width in ((0, N), (0, P), (P, P)):
@@ -107,7 +106,7 @@ def tile_attend_quest_topk_kernel(tc, qT, k_words, k_scales, c_words, c_scales, 
         def one_pass(table, b, opens):
             tile, first = parts[b]
             if table == 0:
-                words = (kw_first, kw_second)[first // HALF][:, first % HALF : first % HALF + P]
+                words = kw_first[:] if first == 0 else kw_second[:, first - P : first]
             else:
                 words = cw_got[:, first : first + P]
             rows = slice(table * NQ + tile * P, table * NQ + (tile + 1) * P)

@@ -28,12 +28,12 @@ def tile_attend_quest_topk_kernel(tc, qT, k_words, k_scales, c_words, c_scales, 
         keep = ctx.enter_context(tc.tile_pool(name="keep", bufs=1))
         psum = ctx.enter_context(tc.psum_pool(name="psum", bufs=1))
 
-        offsets = keep.tile([P, LIST_COLS], U16, name="offsets")
-        ks_pool = keep.tile([P, T], U8, name="ks_pool", align_bytes=64)
-        cs_pool = keep.tile([P, T], U8, name="cs_pool", align_bytes=64)
-        q_raw = keep.tile([P, PACK * NQ], F32, name="q_raw", tag="q_raw", align_bytes=64)
-        kw_pool = keep.tile([P, T], I32, name="kw_pool", align_bytes=64)
-        cw_pool = keep.tile([P, T], I32, name="cw_pool", align_bytes=64)
+        offsets = keep.tile([P, LIST_COLS], U16, name="offsets", align_bytes=256)
+        ks_pool = keep.tile([P, T], U8, name="ks_pool", align_bytes=256)
+        cs_pool = keep.tile([P, T], U8, name="cs_pool", align_bytes=256)
+        q_raw = keep.tile([P, PACK * NQ], F32, name="q_raw", tag="q_raw", align_bytes=256)
+        kw_pool = keep.tile([P, T], I32, name="kw_pool", align_bytes=256)
+        cw_pool = keep.tile([P, T], I32, name="cw_pool", align_bytes=256)
 
         step = 8
         c_first = 4
@@ -46,7 +46,7 @@ def tile_attend_quest_topk_kernel(tc, qT, k_words, k_scales, c_words, c_scales, 
         nc.sync.dma_start(kw_pool[:], k_words[0].rearrange("p t r -> p (t r)").bitcast(I32))
         nc.sync.dma_start(cw_pool[:], c_words[0].rearrange("p t r -> p (t r)").bitcast(I32))
 
-        bytes_got = keep.tile([P, 2 * N], U8, name="bytes_got", align_bytes=64)
+        bytes_got = keep.tile([P, 2 * N], U8, name="bytes_got", align_bytes=256)
         nc.vector.tensor_copy(bytes_got[:, 0:N], ks_pool[:].indirect(offsets[:]))
         nc.vector.tensor_copy(bytes_got[:, N : 2 * N], cs_pool[:].indirect(offsets[:]))
 
@@ -55,14 +55,14 @@ def tile_attend_quest_topk_kernel(tc, qT, k_words, k_scales, c_words, c_scales, 
             for row in range(1, 4):
                 nc.sync.dma_start(plane[first + row : P : 32, :].bitcast(I32), got[first + step * row : P : 32, :].bitcast(I32))
 
-        hi = keep.tile([P, NQ * PACK], BF16, name="hi", align_bytes=64)
-        lo = keep.tile([P, NQ * PACK], BF16, name="lo", align_bytes=64)
+        hi = keep.tile([P, NQ * PACK], BF16, name="hi", align_bytes=256)
+        lo = keep.tile([P, NQ * PACK], BF16, name="lo", align_bytes=256)
         q_walk = q_raw[:].rearrange("p (t c i) -> p c t i", t=PACK, i=4)
         lo_walk = lo[:].rearrange("p (c i t) -> p c t i", t=PACK, i=4)
         cut = 16
         nc.vector.tensor_scalar_min(lo_walk[:, 0:cut], q_walk[:, 0:cut], 0.0)
         piece = (NQ // 4 - cut) // 2
-        negs = [keep.tile([P, piece * 16], F32, name="neg%d" % i, tag="neg%d" % i, align_bytes=64) for i in range(2)]
+        negs = [keep.tile([P, piece * 16], F32, name="neg%d" % i, tag="neg%d" % i, align_bytes=256) for i in range(2)]
         for i in range(2):
             first = cut + i * piece
             nc.scalar.activation(negs[i][:].rearrange("p (c i t) -> p c t i", t=PACK, i=4), q_walk[:, first : first + piece], relu, scale=-1.0)
@@ -71,21 +71,21 @@ def tile_attend_quest_topk_kernel(tc, qT, k_words, k_scales, c_words, c_scales, 
             nc.scalar.mul(lo[:, first * 16 : (first + piece) * 16], negs[i][:], -1.0)
         nc.scalar.activation(hi[:].rearrange("p (c i t) -> p c t i", t=PACK, i=4), q_walk, relu)
 
-        k_plane = keep.tile([P, N], U8, name="k_plane", tag="neg0", align_bytes=64)
+        k_plane = keep.tile([P, N], U8, name="k_plane", tag="neg0", align_bytes=256)
         place_rows(k_plane, bytes_got[:, 0:N], 0)
 
-        q_codes = keep.tile([P, 2 * NQ], U32, name="q_codes", align_bytes=64)
-        q_scales = keep.tile([P, 2 * NQ], U8, name="q_scales", align_bytes=64)
+        q_codes = keep.tile([P, 2 * NQ], U32, name="q_codes", align_bytes=256)
+        q_scales = keep.tile([P, 2 * NQ], U8, name="q_scales", align_bytes=256)
         nc.vector.quantize_mx(out=q_codes[:, NQ:].bitcast(FP8X4), scales=q_scales[:, NQ:], in_=lo[:])
 
-        c_plane = keep.tile([P, N], U8, name="c_plane", tag="neg1", align_bytes=64)
+        c_plane = keep.tile([P, N], U8, name="c_plane", tag="neg1", align_bytes=256)
         place_rows(c_plane, bytes_got[:, N : 2 * N], c_first)
 
-        kw_first = keep.tile([P, P], U32, name="kw_first", align_bytes=64)
-        cw_got = keep.tile([P, N], U32, name="cw_got", align_bytes=64)
+        kw_first = keep.tile([P, P], U32, name="kw_first", align_bytes=256)
+        cw_got = keep.tile([P, N], U32, name="cw_got", align_bytes=256)
         nc.vector.tensor_copy(kw_first[:], kw_pool[:].bitcast(U32).indirect(offsets[:, 0 : P // 16]))
         nc.vector.quantize_mx(out=q_codes[:, 0:NQ].bitcast(FP8X4), scales=q_scales[:, 0:NQ], in_=hi[:])
-        kw_second = keep.tile([P, N - P], U32, name="kw_second", tag="q_raw", align_bytes=64)
+        kw_second = keep.tile([P, N - P], U32, name="kw_second", tag="q_raw", align_bytes=256)
         nc.vector.tensor_copy(kw_second[:], kw_pool[:].bitcast(U32).indirect(offsets[:, P // 16 :]))
 
         warm = psum.tile([WARM_ROWS, N], F32, name="warm", tag="bank7")
@@ -133,7 +133,7 @@ def tile_attend_quest_topk_kernel(tc, qT, k_words, k_scales, c_words, c_scales, 
 
         for store in range(4):
             tile, first = parts[2 * store]
-            result = keep.tile([P, HALF], F32, name="result%d" % store)
+            result = keep.tile([P, HALF], F32, name="result%d" % store, align_bytes=256)
             for piece in range(2):
                 if store == 2:
                     nc.vector.tensor_copy(result[:, piece * P : (piece + 1) * P], banks[2 * store + piece][:])

@@ -29,11 +29,11 @@ def tile_attend_quest_topk_kernel(tc, qT, k_words, k_scales, c_words, c_scales, 
         psum = ctx.enter_context(tc.psum_pool(name="psum", bufs=1))
 
         offsets = keep.tile([P, LIST_COLS], U16, name="offsets", align_bytes=256)
-        ks_pool = keep.tile([P, T], U8, name="ks_pool", align_bytes=256)
-        cs_pool = keep.tile([P, T], U8, name="cs_pool", align_bytes=256)
-        q_raw = keep.tile([P, PACK * NQ], F32, name="q_raw", tag="q_raw", align_bytes=256)
-        kw_pool = keep.tile([P, T], I32, name="kw_pool", align_bytes=256)
-        cw_pool = keep.tile([P, T], I32, name="cw_pool", align_bytes=256)
+        ks_pool = keep.tile([P, T], U8, name="ks_pool", align_bytes=2048)
+        cs_pool = keep.tile([P, T], U8, name="cs_pool", align_bytes=2048)
+        q_raw = keep.tile([P, PACK * NQ], F32, name="q_raw", tag="q_raw", align_bytes=4096)
+        kw_pool = keep.tile([P, T], I32, name="kw_pool", align_bytes=4096)
+        cw_pool = keep.tile([P, T], I32, name="cw_pool", align_bytes=4096)
 
         step = 8
         c_first = 4
@@ -85,7 +85,7 @@ def tile_attend_quest_topk_kernel(tc, qT, k_words, k_scales, c_words, c_scales, 
         cw_got = keep.tile([P, N], U32, name="cw_got", align_bytes=256)
         nc.vector.tensor_copy(kw_first[:], kw_pool[:].bitcast(U32).indirect(offsets[:, 0 : P // 16]))
         nc.vector.quantize_mx(out=q_codes[:, 0:NQ].bitcast(FP8X4), scales=q_scales[:, 0:NQ], in_=hi[:])
-        kw_second = keep.tile([P, N - P], U32, name="kw_second", tag="q_raw", align_bytes=256)
+        kw_second = keep.tile([P, N - P], U32, name="kw_second", tag="q_raw", align_bytes=4096)
         nc.vector.tensor_copy(kw_second[:], kw_pool[:].bitcast(U32).indirect(offsets[:, P // 16 :]))
 
         warm = psum.tile([WARM_ROWS, N], F32, name="warm", tag="bank7")
@@ -133,7 +133,7 @@ def tile_attend_quest_topk_kernel(tc, qT, k_words, k_scales, c_words, c_scales, 
 
         for store in range(4):
             tile, first = parts[2 * store]
-            result = keep.tile([P, HALF], F32, name="result%d" % store, align_bytes=256)
+            result = keep.tile([P, HALF], F32, name="result%d" % store, align_bytes=1024)
             for piece in range(2):
                 if store == 2:
                     nc.vector.tensor_copy(result[:, piece * P : (piece + 1) * P], banks[2 * store + piece][:])

@@ -100,7 +100,7 @@ def tile_attend_quest_topk_kernel(tc, qT, k_words, k_scales, c_words, c_scales, 
                 stop=True,
             )
 
-        parts = [(tile, half * HALF + piece * P) for half in range(2) for tile in range(2) for piece in range(2)]
+        parts = [(tile, first) for first in range(0, N, P) for tile in range(2)]
         banks = [psum.tile([P, P], F32, name="bank%d" % b, tag="bank%d" % b) for b in range(len(parts))]
 
         def one_pass(table, b, opens):
@@ -122,7 +122,7 @@ def tile_attend_quest_topk_kernel(tc, qT, k_words, k_scales, c_words, c_scales, 
 
         for first in range(0, N, P):
             nc.vector.tensor_copy(cw_got[:, first : first + P], cw_pool[:].bitcast(U32).indirect(offsets[:, first // 16 : (first + P) // 16]))
-        early = 4
+        early = 3
         for b in range(early):
             one_pass(0, b, True)
         for b in range(early):
@@ -131,12 +131,12 @@ def tile_attend_quest_topk_kernel(tc, qT, k_words, k_scales, c_words, c_scales, 
             one_pass(1, b, True)
             one_pass(0, b, False)
 
+        out_tiles = out[0].rearrange("(t p) n -> p t n", p=P)
         for store in range(4):
-            tile, first = parts[2 * store]
-            result = keep.tile([P, HALF], F32, name="result%d" % store, align_bytes=1024)
-            for piece in range(2):
-                if store == 2:
-                    nc.vector.tensor_copy(result[:, piece * P : (piece + 1) * P], banks[2 * store + piece][:])
+            result = keep.tile([P, 2 * P], F32, name="result%d" % store, align_bytes=1024)
+            for tile in range(2):
+                if store >= 2 and tile == 0:
+                    nc.vector.tensor_copy(result[:, tile * P : (tile + 1) * P], banks[2 * store + tile][:])
                 else:
-                    nc.scalar.copy(result[:, piece * P : (piece + 1) * P], banks[2 * store + piece][:])
-            nc.sync.dma_start(out[0, tile * P : (tile + 1) * P, first : first + HALF], result[:])
+                    nc.scalar.copy(result[:, tile * P : (tile + 1) * P], banks[2 * store + tile][:])
+            nc.sync.dma_start(out_tiles[:, :, store * P : (store + 1) * P], result[:].rearrange("p (t n) -> p t n", t=2))

@@ -50,10 +50,10 @@ def tile_attend_quest_topk_kernel(tc, qT, k_words, k_scales, c_words, c_scales, 
         nc.vector.tensor_copy(bytes_got[:, 0:N], ks_pool[:].indirect(offsets[:]))
         nc.vector.tensor_copy(bytes_got[:, N : 2 * N], cs_pool[:].indirect(offsets[:]))
 
-        def place_rows(plane, got, first):
+        def place_rows(plane, got, first, queues):
             nc.vector.tensor_copy(plane[:].bitcast(I32), got.bitcast(I32))
-            for row in range(1, 4):
-                nc.sync.dma_start(plane[first + row : P : 32, :].bitcast(I32), got[first + step * row : P : 32, :].bitcast(I32))
+            for row, queue in zip(range(1, 4), queues):
+                queue.dma_start(plane[first + row : P : 32, :].bitcast(I32), got[first + step * row : P : 32, :].bitcast(I32))
 
         hi = keep.tile([P, NQ * PACK], BF16, name="hi", align_bytes=256)
         lo = keep.tile([P, NQ * PACK], BF16, name="lo", align_bytes=256)
@@ -72,14 +72,14 @@ def tile_attend_quest_topk_kernel(tc, qT, k_words, k_scales, c_words, c_scales, 
         nc.scalar.activation(hi[:].rearrange("p (c i t) -> p c t i", t=PACK, i=4), q_walk, relu)
 
         k_plane = keep.tile([P, N], U8, name="k_plane", tag="neg0", align_bytes=256)
-        place_rows(k_plane, bytes_got[:, 0:N], 0)
+        place_rows(k_plane, bytes_got[:, 0:N], 0, (nc.sync, nc.sync, nc.sync))
 
         q_codes = keep.tile([P, 2 * NQ], U32, name="q_codes", align_bytes=256)
         q_scales = keep.tile([P, 2 * NQ], U8, name="q_scales", align_bytes=256)
         nc.vector.quantize_mx(out=q_codes[:, NQ:].bitcast(FP8X4), scales=q_scales[:, NQ:], in_=lo[:])
 
         c_plane = keep.tile([P, N], U8, name="c_plane", tag="neg1", align_bytes=256)
-        place_rows(c_plane, bytes_got[:, N : 2 * N], c_first)
+        place_rows(c_plane, bytes_got[:, N : 2 * N], c_first, (nc.scalar, nc.scalar, nc.sync))
 
         kw_first = keep.tile([P, P], U32, name="kw_first", align_bytes=256)
         cw_got = keep.tile([P, N], U32, name="cw_got", align_bytes=256)
@@ -122,7 +122,7 @@ def tile_attend_quest_topk_kernel(tc, qT, k_words, k_scales, c_words, c_scales, 
 
         for first in range(0, N, P):
             nc.vector.tensor_copy(cw_got[:, first : first + P], cw_pool[:].bitcast(U32).indirect(offsets[:, first // 16 : (first + P) // 16]))
-        early = 3
+        early = 4
         for b in range(early):
             one_pass(0, b, True)
         for b in range(early):

from contextlib import ExitStack

import concourse.mybir as mybir

D, NQ, T, N = 512, 256, 2048, 512
FLOPS = 2 * 2 * D * NQ * N

F32 = mybir.dt.float32
BF16 = mybir.dt.bfloat16
I32 = mybir.dt.int32
U32 = mybir.dt.uint32
U16 = mybir.dt.uint16
U8 = mybir.dt.uint8
FP8X4 = mybir.dt.float8_e4m3fn_x4

P = 128
PACK = 4
ROWS = 16
HALF = N // 2
LIST_COLS = N // 16
WARM_ROWS = 32


def tile_attend_quest_topk_kernel(tc, qT, k_words, k_scales, c_words, c_scales, offs, out):
    nc = tc.nc
    relu = mybir.ActivationFunctionType.Relu
    with ExitStack() as ctx:
        keep = ctx.enter_context(tc.tile_pool(name="keep", bufs=1))
        psum = ctx.enter_context(tc.psum_pool(name="psum", bufs=1))

        offsets = keep.tile([P, LIST_COLS], U16, name="offsets", align_bytes=256)
        ks_pool = keep.tile([P, T], U8, name="ks_pool", align_bytes=2048)
        cs_pool = keep.tile([P, T], U8, name="cs_pool", align_bytes=2048)
        q_raw = keep.tile([P, PACK * NQ], F32, name="q_raw", tag="q_raw", align_bytes=4096)
        kw_pool = keep.tile([P, T], I32, name="kw_pool", align_bytes=4096)
        cw_pool = keep.tile([P, T], I32, name="cw_pool", align_bytes=4096)

        step = 8
        c_first = 4
        nc.vector.memset(ks_pool[:].bitcast(I32), 0)
        nc.vector.memset(cs_pool[:].bitcast(I32), 0)
        nc.sync.dma_start(q_raw[:], qT[0].rearrange("(p j) w -> p (j w)", j=PACK))
        nc.sync.dma_start(offsets[:], offs)
        nc.sync.dma_start(ks_pool[0:P:step, :].bitcast(I32), k_scales[0].bitcast(I32))
        nc.sync.dma_start(cs_pool[c_first:P:step, :].bitcast(I32), c_scales[0].bitcast(I32))
        nc.sync.dma_start(kw_pool[:], k_words[0].rearrange("p t r -> p (t r)").bitcast(I32))
        nc.sync.dma_start(cw_pool[:], c_words[0].rearrange("p t r -> p (t r)").bitcast(I32))

        bytes_got = keep.tile([P, 2 * N], U8, name="bytes_got", align_bytes=256)
        nc.vector.tensor_copy(bytes_got[:, 0:N], ks_pool[:].indirect(offsets[:]))
        nc.vector.tensor_copy(bytes_got[:, N : 2 * N], cs_pool[:].indirect(offsets[:]))

        def place_rows(plane, got, first, queues):
            nc.vector.tensor_copy(plane[:].bitcast(I32), got.bitcast(I32))
            for row, queue in zip(range(1, 4), queues):
                queue.dma_start(plane[first + row : P : 32, :].bitcast(I32), got[first + step * row : P : 32, :].bitcast(I32))

        hi = keep.tile([P, NQ * PACK], BF16, name="hi", align_bytes=256)
        lo = keep.tile([P, NQ * PACK], BF16, name="lo", align_bytes=256)
        q_walk = q_raw[:].rearrange("p (t c i) -> p c t i", t=PACK, i=4)
        lo_walk = lo[:].rearrange("p (c i t) -> p c t i", t=PACK, i=4)
        cut = 16
        nc.vector.tensor_scalar_min(lo_walk[:, 0:cut], q_walk[:, 0:cut], 0.0)
        piece = (NQ // 4 - cut) // 2
        negs = [keep.tile([P, piece * 16], F32, name="neg%d" % i, tag="neg%d" % i, align_bytes=256) for i in range(2)]
        for i in range(2):
            first = cut + i * piece
            nc.scalar.activation(negs[i][:].rearrange("p (c i t) -> p c t i", t=PACK, i=4), q_walk[:, first : first + piece], relu, scale=-1.0)
        for i in range(2):
            first = cut + i * piece
            nc.scalar.mul(lo[:, first * 16 : (first + piece) * 16], negs[i][:], -1.0)
        nc.scalar.activation(hi[:].rearrange("p (c i t) -> p c t i", t=PACK, i=4), q_walk, relu)

        k_plane = keep.tile([P, N], U8, name="k_plane", tag="neg0", align_bytes=256)
        place_rows(k_plane, bytes_got[:, 0:N], 0, (nc.sync, nc.sync, nc.sync))

        q_codes = keep.tile([P, 2 * NQ], U32, name="q_codes", align_bytes=256)
        q_scales = keep.tile([P, 2 * NQ], U8, name="q_scales", align_bytes=256)
        nc.vector.quantize_mx(out=q_codes[:, NQ:].bitcast(FP8X4), scales=q_scales[:, NQ:], in_=lo[:])

        c_plane = keep.tile([P, N], U8, name="c_plane", tag="neg1", align_bytes=256)
        place_rows(c_plane, bytes_got[:, N : 2 * N], c_first, (nc.scalar, nc.scalar, nc.sync))

        kw_first = keep.tile([P, P], U32, name="kw_first", align_bytes=256)
        cw_got = keep.tile([P, N], U32, name="cw_got", align_bytes=256)
        nc.vector.tensor_copy(kw_first[:], kw_pool[:].bitcast(U32).indirect(offsets[:, 0 : P // 16]))
        nc.vector.quantize_mx(out=q_codes[:, 0:NQ].bitcast(FP8X4), scales=q_scales[:, 0:NQ], in_=hi[:])
        kw_second = keep.tile([P, N - P], U32, name="kw_second", tag="q_raw", align_bytes=4096)
        nc.vector.tensor_copy(kw_second[:], kw_pool[:].bitcast(U32).indirect(offsets[:, P // 16 :]))

        warm = psum.tile([WARM_ROWS, N], F32, name="warm", tag="bank7")
        for first, width in ((0, N), (0, P), (P, P)):
            nc.tensor.matmul_mx(
                out=warm[:, 0:width],
                lhsT=q_codes[:, 0:WARM_ROWS].bitcast(FP8X4),
                lhsT_scale=q_scales[:, 0:WARM_ROWS],
                rhs=q_codes[:, first : first + width].bitcast(FP8X4),
                rhs_scale=q_scales[:, first : first + width],
                start=True,
                stop=True,
            )

        parts = [(tile, first) for first in range(0, N, P) for tile in range(2)]
        banks = [psum.tile([P, P], F32, name="bank%d" % b, tag="bank%d" % b) for b in range(len(parts))]

        def one_pass(table, b, opens):
            tile, first = parts[b]
            if table == 0:
                words = kw_first[:] if first == 0 else kw_second[:, first - P : first]
            else:
                words = cw_got[:, first : first + P]
            rows = slice(table * NQ + tile * P, table * NQ + (tile + 1) * P)
            nc.tensor.matmul_mx(
                out=banks[b][:],
                lhsT=q_codes[:, rows].bitcast(FP8X4),
                lhsT_scale=q_scales[:, rows],
                rhs=words.bitcast(FP8X4),
                rhs_scale=(k_plane[:], c_plane[c_first:P, :])[table][:, first : first + P],
                start=opens,
                stop=not opens,
            )

        for first in range(0, N, P):
            nc.vector.tensor_copy(cw_got[:, first : first + P], cw_pool[:].bitcast(U32).indirect(offsets[:, first // 16 : (first + P) // 16]))
        early = 4
        for b in range(early):
            one_pass(0, b, True)
        for b in range(early):
            one_pass(1, b, False)
        for b in range(early, len(parts)):
            one_pass(1, b, True)
            one_pass(0, b, False)

        out_tiles = out[0].rearrange("(t p) n -> p t n", p=P)
        for store in range(4):
            result = keep.tile([P, 2 * P], F32, name="result%d" % store, align_bytes=1024)
            for tile in range(2):
                if store >= 2 and tile == 0:
                    nc.vector.tensor_copy(result[:, tile * P : (tile + 1) * P], banks[2 * store + tile][:])
                else:
                    nc.scalar.copy(result[:, tile * P : (tile + 1) * P], banks[2 * store + tile][:])
            nc.sync.dma_start(out_tiles[:, :, store * P : (store + 1) * P], result[:].rearrange("p (t n) -> p t n", t=2))
